import numpy as np
import ml_dtypes


def mxq(x, axis, fmt="e4m3"):
    dtype, down = {"e4m3": (ml_dtypes.float8_e4m3fn, 7), "e5m2": (ml_dtypes.float8_e5m2, 14)}[fmt]
    v = np.moveaxis(np.asarray(x, np.float32).astype(ml_dtypes.bfloat16).astype(np.float64), axis, -1)
    blocks = v.reshape(v.shape[:-1] + (-1, 32))
    amax = np.abs(blocks).max(-1, keepdims=True)
    byte = np.maximum(np.where(amax > 0, np.frexp(amax)[1] - 1 + 127, 0) - down, 1)
    scale = np.exp2(byte - 127.0)
    codes = (blocks / scale).astype(np.float32).astype(dtype).astype(np.float64)
    return np.moveaxis((codes * scale).reshape(v.shape), -1, axis)


WIDE = False


def mx_kscale(k):
    if not WIDE:
        return np.ones(k)
    levels = np.array([10, -10, 5, -5, 0])
    if k % 512:
        return np.exp2(np.random.permutation(np.resize(levels, k // 32))).repeat(32)
    a = np.empty((k // 512, 16))
    for p in range(k // 512):
        a[p, :8] = np.random.permutation(np.resize(levels, 8))
        for g in range(8):
            far = levels[np.abs(levels - a[p, g]) >= 10]
            a[p, g + 8] = far[np.random.randint(len(far))]
    return np.exp2(a.ravel()).repeat(32)


BF16 = ml_dtypes.bfloat16


def bf(x):
    return np.asarray(x, np.float32).astype(BF16)


def f64(x):
    return np.asarray(x).astype(np.float64)


E2M1 = np.array([0.0, 0.5, 1.0, 1.5, 2.0, 3.0, 4.0, 6.0, -0.0, -0.5, -1.0, -1.5, -2.0, -3.0, -4.0, -6.0])


def pack_weight(w, fmt):
    k, n = w.shape
    w = f64(bf(w)).reshape(k // 32, 32, n)
    amax = np.abs(w).max(1)
    if fmt == "e4m3":
        byte = np.frexp(amax)[1] - 1 + 127 - 7
    else:
        mant, ex = np.frexp(amax / 6.0)
        byte = np.where(mant > 0.5, ex, ex - 1) + 127
    byte = np.clip(np.where(amax > 0, byte, 1), 1, 254)
    scaled = (w * np.exp2(127.0 - byte)[:, None, :]).reshape(k, n).astype(np.float32)
    by_word = np.ascontiguousarray(scaled.reshape(k // 512, 128, 4, n).transpose(0, 1, 3, 2))
    if fmt == "e4m3":
        words = by_word.astype(ml_dtypes.float8_e4m3fn).view(np.uint8)
    else:
        c = by_word.astype(ml_dtypes.float4_e2m1fn).view(np.uint8) & 0xF
        words = c[..., 0::2] | (c[..., 1::2] << 4)
    return np.ascontiguousarray(words), np.ascontiguousarray(byte.astype(np.uint8).reshape(k // 512, 16, n))


def unpack_weight(words, scales, fmt):
    g, p, n, _ = words.shape
    if fmt == "e4m3":
        vals = np.ascontiguousarray(words).view(ml_dtypes.float8_e4m3fn).astype(np.float64)
    else:
        nib = np.empty((g, p, n, 4), np.uint8)
        nib[..., 0::2] = words & 0xF
        nib[..., 1::2] = words >> 4
        vals = E2M1[nib]
    vals = vals * np.repeat(np.exp2(scales.astype(np.float64) - 127.0), 8, axis=1)[..., None]
    return vals.transpose(0, 1, 3, 2).reshape(g * 512, n)
def pack4(w):
    words, scales = pack_weight(w, "e2m1")
    return words.reshape(words.shape[0], 128, -1), scales


def unpack4(words, scales):
    return unpack_weight(words.reshape(words.shape[0], 128, -1, 2), scales, "e2m1")


N, R = 1536, 512


def setup_inputs():
    s = mx_kscale(N)
    t = mx_kscale(N)
    pt = np.random.standard_normal((N, N)) * s[:, None]
    ov = np.random.standard_normal((N, N)) / np.sqrt(N) / s[:, None]
    w = np.random.standard_normal((N, R)) / np.sqrt(N) / t[:, None]
    pt_words, pt_scales = pack4(pt)
    s_words, s_scales = pack4(ov)
    w_words, w_scales = pack_weight(w, "e4m3")
    return {"pt_words": pt_words, "pt_scales": pt_scales,
            "s_words": s_words, "s_scales": s_scales,
            "v": bf((1 + 0.1 * np.random.standard_normal(N)) * t),
            "w_words": w_words, "w_scales": w_scales,
            "b": bf(0.3 * np.random.standard_normal(R))}


def reference(pt_words, pt_scales, s_words, s_scales, v, w_words, w_scales, b):
    pt = unpack4(pt_words, pt_scales)
    ov = unpack4(s_words, s_scales)
    ps = pt.T @ ov
    bond = ps * ps.T * f64(v)
    w = unpack_weight(w_words, w_scales, "e4m3")
    d = mxq(bond, 1, "e4m3") @ w
    return d + f64(b)

@@ -1,0 +1,445 @@
+from contextlib import ExitStack
+
+import concourse.mybir as mybir
+from concourse.masks import make_identity
+
+N, R = 1536, 512
+FLOPS = 2 * N * N * N + 2 * N * N * R
+
+F32 = mybir.dt.float32
+BF16 = mybir.dt.bfloat16
+I32 = mybir.dt.int32
+U32 = mybir.dt.uint32
+U8 = mybir.dt.uint8
+FP4X4 = mybir.dt.float4_e2m1fn_x4
+FP8X4 = mybir.dt.float8_e4m3fn_x4
+MULT = mybir.AluOpType.mult
+ADD = mybir.AluOpType.add
+COPY = mybir.ActivationFunctionType.Copy
+
+P = 128
+G = 3
+S = 512
+A, B, C = 0, 1, 2
+PT, OV = 0, 1
+BANKS = 8
+
+
+def tile_mayer_bond_orders_s4_kernel(tc, pt_words, pt_scales, s_words, s_scales, v, w_words, w_scales, b, out):
+    nc = tc.nc
+    words_hbm = (pt_words, s_words)
+    scales_hbm = (pt_scales, s_scales)
+
+    with ExitStack() as ctx:
+        keep = ctx.enter_context(tc.tile_pool(name="keep", bufs=1))
+        work = ctx.enter_context(tc.tile_pool(name="work", bufs=1))
+        psum = ctx.enter_context(tc.psum_pool(name="psum", bufs=1))
+        ctx.enter_context(tc.manual_schedule())
+
+        taken = []
+
+        def bank():
+            taken.append(0)
+            return psum.tile([P, S], F32, name="bank%d" % (len(taken) % BANKS))
+
+        codes, planes = {}, {}
+
+        def load_codes(queue, op, sb):
+            t = keep.tile([P, G, 2 * S], U8, name="codes%d%d" % (op, sb), align_bytes=64)
+            src = words_hbm[op][:, :, 2 * S * sb : 2 * S * (sb + 1)].rearrange("g p c -> p g c")
+            queue.dma_start(out=t[:].bitcast(I32), in_=src.bitcast(I32))
+            codes[op, sb] = t
+
+        def blank_plane(engine, name, width):
+            t = keep.tile([P, G, width], U8, name=name, align_bytes=64)
+            engine.memset(t[:].bitcast(I32), 0)
+            return t
+
+        def load_plane(t, hbm, which, queue=nc.sync):
+            rows = hbm.rearrange("g (q r) n -> q r g n", r=4)
+            for r in which:
+                queue.dma_start(out=t[32 * r : 32 * r + 4, :, :].bitcast(I32), in_=rows[r].bitcast(I32))
+
+        late = {}
+        for op in (PT, OV):
+            planes[op, A] = blank_plane(nc.vector, "plane%da" % op, S)[:]
+        ident = keep.tile([P, P], F32, name="ident")
+        make_identity(nc, ident[:])
+        for op in (PT, OV):
+            late[op] = blank_plane(nc.vector, "plane%dbc" % op, 2 * S)
+            planes[op, B], planes[op, C] = late[op][:, :, :S], late[op][:, :, S:]
+        w_plane = blank_plane(nc.gpsimd, "w_plane", R)
+
+        v_nat16 = keep.tile([P, 4, 2], BF16, name="v_nat16")
+        v_slot16 = keep.tile([P, 2, 4], BF16, name="v_slot16")
+        b_slot16 = keep.tile([P, 4], BF16, name="b_slot16")
+        w_codes = keep.tile([P, G, 4 * R], U8, name="w_codes", align_bytes=64)
+
+        load_plane(planes[PT, A], pt_scales[:, :, :S], range(2))
+        load_codes(nc.sync, OV, A)
+        load_codes(nc.sync, PT, A)
+        load_plane(planes[PT, A], pt_scales[:, :, :S], range(2, 4))
+        load_plane(planes[OV, A], s_scales[:, :, :S], range(4))
+        with nc.allow_non_contiguous_dma(reason="one value of v to a partition"):
+            nc.sync.dma_start(out=v_nat16[:, :, 0:1], in_=v[0:S].rearrange("(a p o) -> p a o", p=P, o=1))
+        load_codes(nc.sync, PT, B)
+        load_plane(late[PT], pt_scales[:, :, S:], range(4))
+        load_codes(nc.sync, OV, B)
+        load_plane(late[OV], s_scales[:, :, S:], range(3))
+        load_plane(late[OV], s_scales[:, :, S:], range(3, 4))
+        nc.sync.dma_start(out=v_slot16[:], in_=v[S:N].rearrange("(g p t) -> p g t", p=P, t=4))
+        nc.sync.dma_start(out=b_slot16[:], in_=b.rearrange("(p t) -> p t", t=4))
+        load_codes(nc.sync, PT, C)
+        load_codes(nc.sync, OV, C)
+        load_plane(w_plane, w_scales, range(4))
+        nc.sync.dma_start(out=w_codes[:].bitcast(I32), in_=w_words.rearrange("g p n t -> p g (n t)").bitcast(I32))
+
+        v_nat = keep.tile([P, 4], F32, name="v_nat")
+        v_slot = keep.tile([P, 2, 4], F32, name="v_slot")
+        b_slot = keep.tile([P, 4], F32, name="b_slot")
+        nc.vector.tensor_copy(out=v_nat[:], in_=v_nat16[:, :, 0])
+        nc.gpsimd.tensor_copy(out=v_slot[:], in_=v_slot16[:])
+        nc.gpsimd.tensor_copy(out=b_slot[:], in_=b_slot16[:])
+
+        def v_col(sb, t):
+            return v_slot[:, sb - 1, t : t + 1]
+
+        slot_codes, slot_planes = {}, {}
+
+        def gather_slot(op, sb, t):
+            c = keep.tile([P, G, 2 * P], U8, name="slot_codes%d%d%d" % (op, sb, t), align_bytes=64)
+            s = keep.tile([P, G, P], U8, name="slot_plane%d%d%d" % (op, sb, t), align_bytes=64)
+            nc.vector.tensor_copy(
+                out=c[:].rearrange("q g (m e) -> q g m e", e=2),
+                in_=codes[op, sb][:].rearrange("q g (m t e) -> q t g m e", t=4, e=2)[:, t],
+            )
+            nc.vector.tensor_copy(out=s[:], in_=planes[op, sb].rearrange("q g (m t) -> q t g m", t=4)[:, t])
+            slot_codes[op, sb, t], slot_planes[op, sb, t] = c, s
+
+        def product(op, sb, t, moving_sb):
+            acc = bank()
+            for g in range(G):
+                if sb == A:
+                    lhs = codes[op, sb][:, g, 2 * P * t : 2 * P * (t + 1)]
+                    lhs_scale = planes[op, sb][:, g, P * t : P * (t + 1)]
+                else:
+                    lhs = slot_codes[op, sb, t][:, g, :]
+                    lhs_scale = slot_planes[op, sb, t][:, g, :]
+                nc.tensor.matmul_mx(
+                    out=acc[:],
+                    lhsT=lhs.bitcast(FP4X4),
+                    lhsT_scale=lhs_scale,
+                    rhs=codes[1 - op, moving_sb][:, g, :].bitcast(FP4X4),
+                    rhs_scale=planes[1 - op, moving_sb][:, g, :],
+                    start=(g == 0),
+                    stop=(g == G - 1),
+                )
+            return acc
+
+        def by_word(ap):
+            return ap.rearrange("q (p u e) -> q u p e", u=2, e=2)
+
+        def as_word(ap):
+            return ap.rearrange("q (u p e) -> q u p e", u=2, e=2)
+
+        def spread(cols, name, pattern_in, pattern_out, sizes):
+            acc = bank()
+            for n in range(4):
+                nc.tensor.transpose(acc[:, P * n : P * (n + 1)], cols[:, n : n + 1].to_broadcast([P, P]), ident[:])
+            t = keep.tile([P, S], F32, name=name)
+            return t, lambda: nc.scalar.copy(out=t[:].rearrange(pattern_out, **sizes), in_=acc[:].rearrange(pattern_in, **sizes))
+
+        d_codes, d_planes = {}, {}
+        for g in range(G):
+            for sb in range(G):
+                d_codes[g, sb] = keep.tile([P, S], U32, name="dq%d%d" % (g, sb), align_bytes=64)
+                d_planes[g, sb] = keep.tile([P, S], U8, name="dqs%d%d" % (g, sb), align_bytes=64)
+
+        def quantize(g, sb, first, grouped):
+            n = grouped.shape[1] // 4
+            nc.vector.quantize_mx(
+                out=d_codes[g, sb][:, first : first + n].bitcast(FP8X4),
+                scales=d_planes[g, sb][:, first : first + n],
+                in_=grouped,
+            )
+
+        st = {}
+
+        def word_turn(key, half):
+            acc = bank()
+            for n in range(2):
+                words = st[key, "rows", 2 * half + n][:].bitcast(F32)
+                for u in range(2):
+                    nc.tensor.transpose(acc[:, P * (2 * n + u) : P * (2 * n + u + 1)], words[:, P * u : P * (u + 1)], ident[:])
+            st[key, "turned", half] = acc
+
+        def word_copy(key, half):
+            t = work.tile([P, 2 * S], BF16, name="word_grouped", bufs=4, align_bytes=64)
+            nc.scalar.copy(
+                out=t[:].bitcast(F32).rearrange("q (n r u) -> q n r u", n=2, u=2),
+                in_=st[key, "turned", half][:].rearrange("q (n u r) -> q n r u", n=2, u=2),
+            )
+            st[key, "wg", half] = t
+
+        def word_quantize(key, half, g, sb):
+            quantize(g, sb, 2 * P * half, st[key, "wg", half][:])
+
+        def slots_tile(key):
+            if (key, "slots") not in st:
+                st[key, "slots"] = work.tile([P, 4, S], BF16, name="slots", bufs=3)
+            return st[key, "slots"]
+
+        def interleave(key, n, engine):
+            if n % 2 == 0:
+                st[key, "sg", n // 2] = work.tile([P, 2 * S], BF16, name="slot_grouped", bufs=4, align_bytes=64)
+            src = st[key, "slots"][:, :, P * n : P * (n + 1)].rearrange("q t r -> q r t")
+            dst = st[key, "sg", n // 2][:, S * (n % 2) : S * (n % 2 + 1)].rearrange("q (r t) -> q r t", t=4)
+            if engine == "s":
+                nc.scalar.copy(out=dst, in_=src)
+            else:
+                nc.vector.tensor_copy(out=dst, in_=src)
+
+        def slot_quantize(key, half, g, sb):
+            quantize(g, sb, 2 * P * half, st[key, "sg", half][:])
+
+        def a_mm(t):
+            st["A", "acc", t] = product(PT, A, t, A)
+
+        def a_scaled(t):
+            x = work.tile([P, S], F32, name="diag_t", bufs=4)
+            nc.scalar.activation(out=x[:], in_=st["A", "acc", t][:], func=COPY, scale=v_nat[:, t : t + 1])
+            st["A", "scaled", t] = x
+
+        def a_plain(t):
+            x = work.tile([P, S], F32, name="a_plain", bufs=4)
+            nc.scalar.copy(out=as_word(x[:]), in_=by_word(st["A", "acc", t][:]))
+            st["A", "plain", t] = x
+
+        def turn(key, name, t):
+            acc = bank()
+            for n in range(4):
+                nc.tensor.transpose(acc[:, P * n : P * (n + 1)], st[key, name, n][:, P * t : P * (t + 1)], ident[:])
+            st[key, "mirror", t] = acc
+
+        def a_bond(t):
+            x = work.tile([P, S], BF16, name="rows", bufs=8)
+            nc.vector.tensor_tensor(out=as_word(x[:]), in0=by_word(st["A", "mirror", t][:]), in1=as_word(st["A", "plain", t][:]), op=MULT)
+            st["A", "rows", t] = x
+
+        def d_mm(sb, t):
+            st[sb, "acc", t] = product(PT, sb, t, sb)
+
+        def d_copy(sb, t):
+            x = work.tile([P, S], F32, name="diag_t", bufs=4)
+            nc.scalar.copy(out=x[:].rearrange("q (t p) -> q t p", t=4), in_=st[sb, "acc", t][:].rearrange("q (p t) -> q t p", t=4))
+            st[sb, "plain", t] = x
+
+        def d_bond(sb, t):
+            nc.vector.scalar_tensor_tensor(
+                out=slots_tile(sb)[:, t, :], in0=st[sb, "mirror", t][:], scalar=v_col(sb, t), in1=st[sb, "plain", t][:], op0=MULT, op1=MULT
+            )
+
+        def p_mm(x, y, t):
+            st[(x, y), "p", t] = product(PT, x, t, y)
+            st[(x, y), "q", t] = product(OV, x, t, y)
+
+        def p_copy(x, y, t):
+            z = work.tile([P, S], F32, name="pair_t", bufs=3)
+            nc.scalar.copy(out=as_word(z[:]), in_=by_word(st[(x, y), "p", t][:]))
+            st[(x, y), "plain", t] = z
+
+        def p_bond(x, y, t):
+            z = work.tile([P, S], F32, name="bond", bufs=4)
+            nc.vector.tensor_tensor(out=as_word(z[:]), in0=by_word(st[(x, y), "q", t][:]), in1=as_word(st[(x, y), "plain", t][:]), op=MULT)
+            st[(x, y), "bond", t] = z
+
+        def p_rows(x, y, t):
+            z = work.tile([P, S], BF16, name="rows", bufs=8)
+            nc.vector.tensor_tensor(out=z[:], in0=st[(x, y), "bond", t][:], in1=st["v_row", y][:], op=MULT)
+            st[(x, y), "rows", t] = z
+
+        def p_slot(x, y, t):
+            order = "p u e" if y == A else "u e p"
+            sizes = dict(u=2, e=2)
+            nc.scalar.activation(
+                out=slots_tile((x, y))[:, t, :].rearrange("q (%s) -> q %s" % (order, order), **sizes),
+                in_=st[(x, y), "bond", t][:].rearrange("q (u p e) -> q %s" % order, **sizes),
+                func=COPY,
+                scale=v_col(x, t),
+            )
+
+        def o_mm(sb, t):
+            acc = bank()
+            for g in range(G):
+                nc.tensor.matmul_mx(
+                    out=acc[:],
+                    lhsT=d_codes[g, sb][:, P * t : P * (t + 1)].bitcast(FP8X4),
+                    lhsT_scale=d_planes[g, sb][:, P * t : P * (t + 1)],
+                    rhs=w_codes[:, g, :].bitcast(FP8X4),
+                    rhs_scale=w_plane[:, g, :],
+                    start=(g == 0),
+                    stop=(g == G - 1),
+                )
+            st["out", sb, t] = acc
+
+        def o_store(sb, t):
+            res = work.tile([P, R], F32, name="res", bufs=8)
+            nc.vector.tensor_tensor(out=res[:], in0=st["out", sb, t][:], in1=st["b_row"][:], op=ADD)
+            rows = out[S * sb : S * (sb + 1), :]
+            dst = rows[P * t : P * (t + 1), :] if sb == A else rows.rearrange("(p t) r -> t p r", t=4)[t]
+            nc.sync.dma_start(out=dst, in_=res[:])
+
+
+        word_in, word_out, ue = "q (p u e) -> q u p e", "q (u p e) -> q u p e", dict(u=2, e=2)
+
+        def spread_va():
+            st["v_row", A], copy = spread(v_nat, "v_row_a", word_in, word_out, ue)
+            copy()
+
+        def spread_vc():
+            st["v_row", C], copy = spread(v_slot[:, 1, :], "v_row_c", "q (u e p) -> q u p e", word_out, ue)
+            copy()
+
+        def spread_b():
+            st["b_row"], copy = spread(b_slot, "b_row", "q (t p) -> q p t", "q (p t) -> q p t", dict(t=4))
+            copy()
+
+        def pair_step(x, y, t):
+            p_mm(x, y, t)
+            p_copy(x, y, t)
+            if t > 0:
+                p_slot(x, y, t - 1)
+
+        def word_both(key):
+            word_turn(key, 0)
+            word_turn(key, 1)
+
+        for t in range(4):
+            a_mm(t)
+            a_scaled(t)
+            if t < 2:
+                a_plain(t)
+        for op, t in ((PT, 0), (PT, 1), (OV, 0), (OV, 1), (PT, 2), (OV, 2), (PT, 3)):
+            gather_slot(op, B, t)
+        a_plain(2)
+        a_plain(3)
+        pair_step(B, A, 0)
+        spread_va()
+        for t in range(4):
+            turn("A", "scaled", t)
+        p_bond(B, A, 0)
+        a_bond(0)
+        a_bond(1)
+        pair_step(B, A, 1)
+        a_bond(2)
+        a_bond(3)
+        p_bond(B, A, 1)
+        p_rows(B, A, 0)
+        gather_slot(OV, B, 3)
+        pair_step(B, A, 2)
+        p_rows(B, A, 1)
+        word_both("A")
+        spread_vc()
+        p_bond(B, A, 2)
+        word_copy("A", 0)
+        pair_step(B, A, 3)
+        word_copy("A", 1)
+        word_quantize("A", 0, A, A)
+        p_rows(B, A, 2)
+        p_bond(B, A, 3)
+        word_quantize("A", 1, A, A)
+
+        def diag_after_pair(sb, x, y, extra, fill):
+            k = (x, y)
+            d_mm(sb, 0)
+            p_slot(x, y, 3)
+            d_copy(sb, 0)
+            p_rows(x, y, 3)
+            fill(0)
+            d_mm(sb, 1)
+            d_copy(sb, 1)
+            interleave(k, 0, "v")
+            interleave(k, 1, "v")
+            d_mm(sb, 2)
+            d_copy(sb, 2)
+            word_both(k)
+            extra()
+            word_copy(k, 0)
+            slot_quantize(k, 0, x, y)
+            fill(1)
+            d_mm(sb, 3)
+            d_copy(sb, 3)
+            word_copy(k, 1)
+
+        def pair_after_diag(x, y, sb, px, py, fill):
+            k = (px, py)
+            pair_step(x, y, 0)
+            interleave(k, 2, "s")
+            interleave(k, 3, "s")
+            word_quantize(k, 0, py, px)
+            word_quantize(k, 1, py, px)
+            for t in range(4):
+                turn(sb, "plain", t)
+            p_bond(x, y, 0)
+            d_bond(sb, 0)
+            d_bond(sb, 1)
+            pair_step(x, y, 1)
+            d_bond(sb, 2)
+            d_bond(sb, 3)
+            slot_quantize(k, 1, px, py)
+            p_bond(x, y, 1)
+            p_rows(x, y, 0)
+            fill(2)
+            pair_step(x, y, 2)
+            interleave(sb, 0, "s")
+            interleave(sb, 1, "s")
+            p_rows(x, y, 1)
+            p_bond(x, y, 2)
+            slot_quantize(sb, 0, sb, sb)
+            fill(3)
+            pair_step(x, y, 3)
+            interleave(sb, 2, "s")
+            interleave(sb, 3, "s")
+            p_rows(x, y, 2)
+            p_bond(x, y, 3)
+            slot_quantize(sb, 1, sb, sb)
+
+        todo = [(PT, C, t) for t in range(4)] + [(OV, C, t) for t in range(4)]
+        def fill(counts):
+            def f(n):
+                for i in range(counts[n]):
+                    gather_slot(*todo.pop(0))
+            return f
+        diag_after_pair(B, B, A, spread_b, fill([1, 2]))
+        pair_after_diag(B, C, B, B, A, fill([0, 0, 1, 1]))
+        diag_after_pair(C, B, C, lambda: None, fill([1, 2]))
+        pair_after_diag(C, A, C, B, C, fill([0, 0, 0, 0]))
+        k = (C, A)
+        word_turn(k, 0)
+        p_slot(C, A, 3)
+        word_copy(k, 0)
+        o_mm(B, 0)
+        p_rows(C, A, 3)
+        o_mm(B, 1)
+        interleave(k, 0, "s")
+        interleave(k, 1, "v")
+        word_quantize(k, 0, A, C)
+        o_store(B, 0)
+        o_mm(B, 2)
+        word_turn(k, 1)
+        interleave(k, 2, "s")
+        word_copy(k, 1)
+        slot_quantize(k, 0, C, A)
+        o_store(B, 1)
+        interleave(k, 3, "s")
+        o_mm(B, 3)
+        o_store(B, 2)
+        word_quantize(k, 1, A, C)
+        o_mm(C, 0)
+        slot_quantize(k, 1, C, A)
+        o_store(B, 3)
+        rows = [(C, 0), (C, 1), (A, 0), (A, 1), (C, 2), (C, 3), (A, 2), (A, 3)]
+        for n in range(1, 8):
+            o_mm(*rows[n])
+            o_store(*rows[n - 1])
+        o_store(*rows[-1])

@@ -63,6 +63,9 @@ def tile_mayer_bond_orders_s4_kernel(tc, pt_words, pt_scales, s_words, s_scales,
         late = {}
         for op in (PT, OV):
             planes[op, A] = blank_plane(nc.vector, "plane%da" % op, S)[:]
+        v_nat16 = keep.tile([P, 4, 2], BF16, name="v_nat16")
+        with nc.allow_non_contiguous_dma(reason="one value of v to a partition"):
+            nc.gpsimd.dma_start(out=v_nat16[:, :, 0:1], in_=v[0:S].rearrange("(a p o) -> p a o", p=P, o=1))
         ident = keep.tile([P, P], F32, name="ident")
         make_identity(nc, ident[:])
         for op in (PT, OV):
@@ -70,7 +73,6 @@ def tile_mayer_bond_orders_s4_kernel(tc, pt_words, pt_scales, s_words, s_scales,
             planes[op, B], planes[op, C] = late[op][:, :, :S], late[op][:, :, S:]
         w_plane = blank_plane(nc.gpsimd, "w_plane", R)
 
-        v_nat16 = keep.tile([P, 4, 2], BF16, name="v_nat16")
         v_slot16 = keep.tile([P, 2, 4], BF16, name="v_slot16")
         b_slot16 = keep.tile([P, 4], BF16, name="b_slot16")
         w_codes = keep.tile([P, G, 4 * R], U8, name="w_codes", align_bytes=64)
@@ -80,15 +82,13 @@ def tile_mayer_bond_orders_s4_kernel(tc, pt_words, pt_scales, s_words, s_scales,
         load_codes(nc.sync, PT, A)
         load_plane(planes[PT, A], pt_scales[:, :, :S], range(2, 4))
         load_plane(planes[OV, A], s_scales[:, :, :S], range(4))
-        with nc.allow_non_contiguous_dma(reason="one value of v to a partition"):
-            nc.sync.dma_start(out=v_nat16[:, :, 0:1], in_=v[0:S].rearrange("(a p o) -> p a o", p=P, o=1))
         load_codes(nc.sync, PT, B)
         load_plane(late[PT], pt_scales[:, :, S:], range(4))
         load_codes(nc.sync, OV, B)
         load_plane(late[OV], s_scales[:, :, S:], range(3))
         load_plane(late[OV], s_scales[:, :, S:], range(3, 4))
-        nc.sync.dma_start(out=v_slot16[:], in_=v[S:N].rearrange("(g p t) -> p g t", p=P, t=4))
-        nc.sync.dma_start(out=b_slot16[:], in_=b.rearrange("(p t) -> p t", t=4))
+        nc.gpsimd.dma_start(out=v_slot16[:], in_=v[S:N].rearrange("(g p t) -> p g t", p=P, t=4))
+        nc.gpsimd.dma_start(out=b_slot16[:], in_=b.rearrange("(p t) -> p t", t=4))
         load_codes(nc.sync, PT, C)
         load_codes(nc.sync, OV, C)
         load_plane(w_plane, w_scales, range(4))
@@ -97,9 +97,11 @@ def tile_mayer_bond_orders_s4_kernel(tc, pt_words, pt_scales, s_words, s_scales,
         v_nat = keep.tile([P, 4], F32, name="v_nat")
         v_slot = keep.tile([P, 2, 4], F32, name="v_slot")
         b_slot = keep.tile([P, 4], F32, name="b_slot")
-        nc.vector.tensor_copy(out=v_nat[:], in_=v_nat16[:, :, 0])
-        nc.gpsimd.tensor_copy(out=v_slot[:], in_=v_slot16[:])
-        nc.gpsimd.tensor_copy(out=b_slot[:], in_=b_slot16[:])
+        nc.scalar.activation(out=v_nat[:], in_=v_nat16[:, :, 0], func=COPY)
+
+        def widen():
+            nc.scalar.activation(out=v_slot[:], in_=v_slot16[:], func=COPY)
+            nc.scalar.activation(out=b_slot[:], in_=b_slot16[:], func=COPY)
 
         def v_col(sb, t):
             return v_slot[:, sb - 1, t : t + 1]
@@ -108,13 +110,15 @@ def tile_mayer_bond_orders_s4_kernel(tc, pt_words, pt_scales, s_words, s_scales,
 
         def gather_slot(op, sb, t):
             c = keep.tile([P, G, 2 * P], U8, name="slot_codes%d%d%d" % (op, sb, t), align_bytes=64)
-            s = keep.tile([P, G, P], U8, name="slot_plane%d%d%d" % (op, sb, t), align_bytes=64)
             nc.vector.tensor_copy(
                 out=c[:].rearrange("q g (m e) -> q g m e", e=2),
                 in_=codes[op, sb][:].rearrange("q g (m t e) -> q t g m e", t=4, e=2)[:, t],
             )
-            nc.vector.tensor_copy(out=s[:], in_=planes[op, sb].rearrange("q g (m t) -> q t g m", t=4)[:, t])
-            slot_codes[op, sb, t], slot_planes[op, sb, t] = c, s
+            slot_codes[op, sb, t] = c
+            if t % 2 == 0:
+                s = keep.tile([P, 2, G, P], U8, name="slot_plane%d%d%d" % (op, sb, t), align_bytes=64)
+                nc.vector.tensor_copy(out=s[:], in_=planes[op, sb].rearrange("q g (m t) -> q t g m", t=4)[:, t : t + 2])
+                slot_planes[op, sb, t], slot_planes[op, sb, t + 1] = s[:, 0], s[:, 1]
 
         def product(op, sb, t, moving_sb):
             acc = bank()
@@ -192,8 +196,8 @@ def tile_mayer_bond_orders_s4_kernel(tc, pt_words, pt_scales, s_words, s_scales,
         def interleave(key, n, engine):
             if n % 2 == 0:
                 st[key, "sg", n // 2] = work.tile([P, 2 * S], BF16, name="slot_grouped", bufs=4, align_bytes=64)
-            src = st[key, "slots"][:, :, P * n : P * (n + 1)].rearrange("q t r -> q r t")
-            dst = st[key, "sg", n // 2][:, S * (n % 2) : S * (n % 2 + 1)].rearrange("q (r t) -> q r t", t=4)
+            src = st[key, "slots"][:, :, P * n : P * (n + 1)].rearrange("q t (c i) -> q c t i", i=4)
+            dst = st[key, "sg", n // 2][:, S * (n % 2) : S * (n % 2 + 1)].rearrange("q (c i t) -> q c t i", i=4, t=4)
             if engine == "s":
                 nc.scalar.copy(out=dst, in_=src)
             else:
@@ -268,24 +272,26 @@ def tile_mayer_bond_orders_s4_kernel(tc, pt_words, pt_scales, s_words, s_scales,
                 scale=v_col(x, t),
             )
 
-        def o_mm(sb, t):
-            acc = bank()
+        def o_mm(sb, t, first=0, width=R):
+            acc = bank()[:][:, :width]
+            cols = slice(first, first + width)
             for g in range(G):
                 nc.tensor.matmul_mx(
-                    out=acc[:],
+                    out=acc,
                     lhsT=d_codes[g, sb][:, P * t : P * (t + 1)].bitcast(FP8X4),
                     lhsT_scale=d_planes[g, sb][:, P * t : P * (t + 1)],
-                    rhs=w_codes[:, g, :].bitcast(FP8X4),
-                    rhs_scale=w_plane[:, g, :],
+                    rhs=w_codes[:, g, :].bitcast(FP8X4)[:, cols],
+                    rhs_scale=w_plane[:, g, cols],
                     start=(g == 0),
                     stop=(g == G - 1),
                 )
-            st["out", sb, t] = acc
+            st["out", sb, t, first] = acc
 
-        def o_store(sb, t):
-            res = work.tile([P, R], F32, name="res", bufs=8)
-            nc.vector.tensor_tensor(out=res[:], in0=st["out", sb, t][:], in1=st["b_row"][:], op=ADD)
-            rows = out[S * sb : S * (sb + 1), :]
+        def o_store(sb, t, first=0, width=R):
+            cols = slice(first, first + width)
+            res = work.tile([P, width], F32, name="res", bufs=8)
+            nc.vector.tensor_tensor(out=res[:], in0=st["out", sb, t, first], in1=st["b_row"][:, cols], op=ADD)
+            rows = out[S * sb : S * (sb + 1), cols]
             dst = rows[P * t : P * (t + 1), :] if sb == A else rows.rearrange("(p t) r -> t p r", t=4)[t]
             nc.sync.dma_start(out=dst, in_=res[:])
 
@@ -314,17 +320,24 @@ def tile_mayer_bond_orders_s4_kernel(tc, pt_words, pt_scales, s_words, s_scales,
             word_turn(key, 0)
             word_turn(key, 1)
 
+        todo = [(PT, C, t) for t in range(4)] + [(OV, C, t) for t in range(4)]
+
+        def fill(count):
+            for i in range(min(count, len(todo))):
+                gather_slot(*todo.pop(0))
+
         for t in range(4):
             a_mm(t)
             a_scaled(t)
             if t < 2:
                 a_plain(t)
-        for op, t in ((PT, 0), (PT, 1), (OV, 0), (OV, 1), (PT, 2), (OV, 2), (PT, 3)):
+        for op, t in ((PT, 0), (PT, 1), (OV, 0), (OV, 1), (PT, 2), (OV, 2), (PT, 3), (OV, 3)):
             gather_slot(op, B, t)
+        spread_va()
         a_plain(2)
         a_plain(3)
+        widen()
         pair_step(B, A, 0)
-        spread_va()
         for t in range(4):
             turn("A", "scaled", t)
         p_bond(B, A, 0)
@@ -335,111 +348,120 @@ def tile_mayer_bond_orders_s4_kernel(tc, pt_words, pt_scales, s_words, s_scales,
         a_bond(3)
         p_bond(B, A, 1)
         p_rows(B, A, 0)
-        gather_slot(OV, B, 3)
         pair_step(B, A, 2)
         p_rows(B, A, 1)
         word_both("A")
         spread_vc()
         p_bond(B, A, 2)
         word_copy("A", 0)
-        pair_step(B, A, 3)
         word_copy("A", 1)
-        word_quantize("A", 0, A, A)
+        fill(1)
+        pair_step(B, A, 3)
         p_rows(B, A, 2)
-        p_bond(B, A, 3)
+        word_quantize("A", 0, A, A)
         word_quantize("A", 1, A, A)
+        fill(1)
+        p_bond(B, A, 3)
 
-        def diag_after_pair(sb, x, y, extra, fill):
+        def diag_after_pair(sb, x, y, extra, eng, before):
             k = (x, y)
             d_mm(sb, 0)
-            p_slot(x, y, 3)
             d_copy(sb, 0)
+            p_slot(x, y, 3)
+            fill(1)
             p_rows(x, y, 3)
-            fill(0)
             d_mm(sb, 1)
             d_copy(sb, 1)
-            interleave(k, 0, "v")
-            interleave(k, 1, "v")
+            before()
+            fill(1)
             d_mm(sb, 2)
             d_copy(sb, 2)
-            word_both(k)
-            extra()
-            word_copy(k, 0)
-            slot_quantize(k, 0, x, y)
+            interleave(k, 0, eng)
             fill(1)
             d_mm(sb, 3)
+            word_both(k)
+            extra()
             d_copy(sb, 3)
+            interleave(k, 1, "v")
+            fill(1)
+            word_copy(k, 0)
             word_copy(k, 1)
 
-        def pair_after_diag(x, y, sb, px, py, fill):
+        def pair_after_diag(x, y, sb, px, py, eng, outs=()):
             k = (px, py)
             pair_step(x, y, 0)
-            interleave(k, 2, "s")
-            interleave(k, 3, "s")
+            interleave(k, 2, eng)
+            interleave(k, 3, eng)
+            fill(2)
+            slot_quantize(k, 0, px, py)
             word_quantize(k, 0, py, px)
-            word_quantize(k, 1, py, px)
             for t in range(4):
                 turn(sb, "plain", t)
             p_bond(x, y, 0)
             d_bond(sb, 0)
             d_bond(sb, 1)
+            word_quantize(k, 1, py, px)
             pair_step(x, y, 1)
             d_bond(sb, 2)
             d_bond(sb, 3)
-            slot_quantize(k, 1, px, py)
             p_bond(x, y, 1)
+            slot_quantize(k, 1, px, py)
             p_rows(x, y, 0)
-            fill(2)
-            pair_step(x, y, 2)
             interleave(sb, 0, "s")
-            interleave(sb, 1, "s")
+            for o in outs[:1]:
+                o_mm(*o)
+                interleave(sb, 1, "s")
+            pair_step(x, y, 2)
             p_rows(x, y, 1)
+            for o in outs[:1]:
+                o_store(*o)
+            if not outs:
+                interleave(sb, 1, "s")
             p_bond(x, y, 2)
-            slot_quantize(sb, 0, sb, sb)
-            fill(3)
-            pair_step(x, y, 3)
             interleave(sb, 2, "s")
-            interleave(sb, 3, "s")
+            for o in outs[1:2]:
+                o_mm(*o)
+                word_turn((x, y), 0)
+                word_copy((x, y), 0)
+                o_store(*o)
+            pair_step(x, y, 3)
             p_rows(x, y, 2)
+            slot_quantize(sb, 0, sb, sb)
+            for o in outs[1:2]:
+                word_quantize((x, y), 0, y, x)
+            interleave(sb, 3, "s")
             p_bond(x, y, 3)
-            slot_quantize(sb, 1, sb, sb)
 
-        todo = [(PT, C, t) for t in range(4)] + [(OV, C, t) for t in range(4)]
-        def fill(counts):
-            def f(n):
-                for i in range(counts[n]):
-                    gather_slot(*todo.pop(0))
-            return f
-        diag_after_pair(B, B, A, spread_b, fill([1, 2]))
-        pair_after_diag(B, C, B, B, A, fill([0, 0, 1, 1]))
-        diag_after_pair(C, B, C, lambda: None, fill([1, 2]))
-        pair_after_diag(C, A, C, B, C, fill([0, 0, 0, 0]))
+        diag_after_pair(B, B, A, spread_b, "s", lambda: None)
+        pair_after_diag(B, C, B, B, A, "s")
+        diag_after_pair(C, B, C, lambda: None, "v", lambda: slot_quantize(B, 1, B, B))
+        pair_after_diag(C, A, C, B, C, "v", [(B, 0), (B, 1)])
         k = (C, A)
-        word_turn(k, 0)
         p_slot(C, A, 3)
-        word_copy(k, 0)
-        o_mm(B, 0)
+        o_mm(B, 2)
+        slot_quantize(C, 1, C, C)
         p_rows(C, A, 3)
-        o_mm(B, 1)
+        o_mm(B, 3)
         interleave(k, 0, "s")
         interleave(k, 1, "v")
-        word_quantize(k, 0, A, C)
-        o_store(B, 0)
-        o_mm(B, 2)
+        o_store(B, 2)
+        o_mm(C, 0)
         word_turn(k, 1)
         interleave(k, 2, "s")
-        word_copy(k, 1)
         slot_quantize(k, 0, C, A)
-        o_store(B, 1)
-        interleave(k, 3, "s")
-        o_mm(B, 3)
-        o_store(B, 2)
-        word_quantize(k, 1, A, C)
-        o_mm(C, 0)
-        slot_quantize(k, 1, C, A)
         o_store(B, 3)
-        rows = [(C, 0), (C, 1), (A, 0), (A, 1), (C, 2), (C, 3), (A, 2), (A, 3)]
-        for n in range(1, 8):
+        o_mm(C, 1)
+        interleave(k, 3, "s")
+        word_copy(k, 1)
+        o_store(C, 0)
+        o_mm(A, 0)
+        slot_quantize(k, 1, C, A)
+        o_store(C, 1)
+        o_mm(A, 1)
+        word_quantize(k, 1, A, C)
+        o_store(A, 0)
+        rows = [(A, 1), (A, 2), (A, 3), (C, 2), (C, 3, 0, 256), (C, 3, 256, 256)]
+        for n in range(1, 6):
             o_mm(*rows[n])
             o_store(*rows[n - 1])
         o_store(*rows[-1])

@@ -23,6 +23,7 @@ S = 512
 A, B, C = 0, 1, 2
 PT, OV = 0, 1
 BANKS = 8
+ASIDE = ()
 
 
 def tile_mayer_bond_orders_s4_kernel(tc, pt_words, pt_scales, s_words, s_scales, v, w_words, w_scales, b, out):
@@ -60,65 +61,70 @@ def tile_mayer_bond_orders_s4_kernel(tc, pt_words, pt_scales, s_words, s_scales,
             for r in which:
                 queue.dma_start(out=t[32 * r : 32 * r + 4, :, :].bitcast(I32), in_=rows[r].bitcast(I32))
 
+        ident = keep.tile([P, P], F32, name="ident")
+        make_identity(nc, ident[:])
         late = {}
         for op in (PT, OV):
             planes[op, A] = blank_plane(nc.vector, "plane%da" % op, S)[:]
-        v_nat16 = keep.tile([P, 4, 2], BF16, name="v_nat16")
-        with nc.allow_non_contiguous_dma(reason="one value of v to a partition"):
-            nc.gpsimd.dma_start(out=v_nat16[:, :, 0:1], in_=v[0:S].rearrange("(a p o) -> p a o", p=P, o=1))
-        ident = keep.tile([P, P], F32, name="ident")
-        make_identity(nc, ident[:])
         for op in (PT, OV):
             late[op] = blank_plane(nc.vector, "plane%dbc" % op, 2 * S)
             planes[op, B], planes[op, C] = late[op][:, :, :S], late[op][:, :, S:]
-        w_plane = blank_plane(nc.gpsimd, "w_plane", R)
+        w_plane = blank_plane(nc.vector, "w_plane", R)
 
+        v_nat16 = keep.tile([P, 4, 2], BF16, name="v_nat16")
         v_slot16 = keep.tile([P, 2, 4], BF16, name="v_slot16")
-        b_slot16 = keep.tile([P, 4], BF16, name="b_slot16")
+        v_c16 = keep.tile([P, S], BF16, name="v_c16")
+        b_row = keep.tile([P, R], BF16, name="b_row")
         w_codes = keep.tile([P, G, 4 * R], U8, name="w_codes", align_bytes=64)
 
-        load_plane(planes[PT, A], pt_scales[:, :, :S], range(2))
+        with nc.allow_non_contiguous_dma(reason="one value of v to a partition"):
+            nc.gpsimd.dma_start(out=v_nat16[:, :, 0:1], in_=v[0:S].rearrange("(a p o) -> p a o", p=P, o=1))
+        nc.gpsimd.dma_start(out=v_slot16[:], in_=v[S:N].rearrange("(g p t) -> p g t", p=P, t=4))
+        load_plane(planes[PT, A], pt_scales[:, :, :S], range(3))
         load_codes(nc.sync, OV, A)
         load_codes(nc.sync, PT, A)
-        load_plane(planes[PT, A], pt_scales[:, :, :S], range(2, 4))
+        load_plane(planes[PT, A], pt_scales[:, :, :S], range(3, 4))
         load_plane(planes[OV, A], s_scales[:, :, :S], range(4))
-        load_codes(nc.sync, PT, B)
-        load_plane(late[PT], pt_scales[:, :, S:], range(4))
-        load_codes(nc.sync, OV, B)
-        load_plane(late[OV], s_scales[:, :, S:], range(3))
-        load_plane(late[OV], s_scales[:, :, S:], range(3, 4))
-        nc.gpsimd.dma_start(out=v_slot16[:], in_=v[S:N].rearrange("(g p t) -> p g t", p=P, t=4))
-        nc.gpsimd.dma_start(out=b_slot16[:], in_=b.rearrange("(p t) -> p t", t=4))
+        for op in (PT, OV):
+            load_codes(nc.sync, op, B)
+        for op in (PT, OV):
+            load_plane(late[op], scales_hbm[op][:, :, S:], range(4))
         load_codes(nc.sync, PT, C)
         load_codes(nc.sync, OV, C)
+        nc.sync.dma_start(out=v_c16[:], in_=v[2 * S :].partition_broadcast(P))
         load_plane(w_plane, w_scales, range(4))
         nc.sync.dma_start(out=w_codes[:].bitcast(I32), in_=w_words.rearrange("g p n t -> p g (n t)").bitcast(I32))
+        nc.sync.dma_start(out=b_row[:], in_=b.partition_broadcast(P))
 
         v_nat = keep.tile([P, 4], F32, name="v_nat")
         v_slot = keep.tile([P, 2, 4], F32, name="v_slot")
-        b_slot = keep.tile([P, 4], F32, name="b_slot")
         nc.scalar.activation(out=v_nat[:], in_=v_nat16[:, :, 0], func=COPY)
 
         def widen():
             nc.scalar.activation(out=v_slot[:], in_=v_slot16[:], func=COPY)
-            nc.scalar.activation(out=b_slot[:], in_=b_slot16[:], func=COPY)
 
         def v_col(sb, t):
             return v_slot[:, sb - 1, t : t + 1]
 
         slot_codes, slot_planes = {}, {}
 
-        def gather_slot(op, sb, t):
+        def gather_codes(op, sb, t):
             c = keep.tile([P, G, 2 * P], U8, name="slot_codes%d%d%d" % (op, sb, t), align_bytes=64)
             nc.vector.tensor_copy(
                 out=c[:].rearrange("q g (m e) -> q g m e", e=2),
                 in_=codes[op, sb][:].rearrange("q g (m t e) -> q t g m e", t=4, e=2)[:, t],
             )
             slot_codes[op, sb, t] = c
+
+        def gather_scales(op, sb, t):
+            s = keep.tile([P, 2, G, P], U8, name="slot_plane%d%d%d" % (op, sb, t), align_bytes=64)
+            nc.vector.tensor_copy(out=s[:], in_=planes[op, sb].rearrange("q g (m t) -> q t g m", t=4)[:, t : t + 2])
+            slot_planes[op, sb, t], slot_planes[op, sb, t + 1] = s[:, 0], s[:, 1]
+
+        def gather_slot(op, sb, t):
+            gather_codes(op, sb, t)
             if t % 2 == 0:
-                s = keep.tile([P, 2, G, P], U8, name="slot_plane%d%d%d" % (op, sb, t), align_bytes=64)
-                nc.vector.tensor_copy(out=s[:], in_=planes[op, sb].rearrange("q g (m t) -> q t g m", t=4)[:, t : t + 2])
-                slot_planes[op, sb, t], slot_planes[op, sb, t + 1] = s[:, 0], s[:, 1]
+                gather_scales(op, sb, t)
 
         def product(op, sb, t, moving_sb):
             acc = bank()
@@ -177,16 +183,19 @@ def tile_mayer_bond_orders_s4_kernel(tc, pt_words, pt_scales, s_words, s_scales,
                     nc.tensor.transpose(acc[:, P * (2 * n + u) : P * (2 * n + u + 1)], words[:, P * u : P * (u + 1)], ident[:])
             st[key, "turned", half] = acc
 
+        def grouped(key, kind):
+            if (key, kind) not in st:
+                st[key, kind] = work.tile([P, 4 * S], BF16, name=kind, bufs=3, align_bytes=64)
+            return st[key, kind]
+
         def word_copy(key, half):
-            t = work.tile([P, 2 * S], BF16, name="word_grouped", bufs=4, align_bytes=64)
             nc.scalar.copy(
-                out=t[:].bitcast(F32).rearrange("q (n r u) -> q n r u", n=2, u=2),
+                out=grouped(key, "by_word")[:, 2 * S * half : 2 * S * (half + 1)].bitcast(F32).rearrange("q (n r u) -> q n r u", n=2, u=2),
                 in_=st[key, "turned", half][:].rearrange("q (n u r) -> q n r u", n=2, u=2),
             )
-            st[key, "wg", half] = t
 
-        def word_quantize(key, half, g, sb):
-            quantize(g, sb, 2 * P * half, st[key, "wg", half][:])
+        def word_quantize(key, g, sb, first=0, tiles=4):
+            quantize(g, sb, P * first, st[key, "by_word"][:, S * first : S * (first + tiles)])
 
         def slots_tile(key):
             if (key, "slots") not in st:
@@ -194,17 +203,15 @@ def tile_mayer_bond_orders_s4_kernel(tc, pt_words, pt_scales, s_words, s_scales,
             return st[key, "slots"]
 
         def interleave(key, n, engine):
-            if n % 2 == 0:
-                st[key, "sg", n // 2] = work.tile([P, 2 * S], BF16, name="slot_grouped", bufs=4, align_bytes=64)
             src = st[key, "slots"][:, :, P * n : P * (n + 1)].rearrange("q t (c i) -> q c t i", i=4)
-            dst = st[key, "sg", n // 2][:, S * (n % 2) : S * (n % 2 + 1)].rearrange("q (c i t) -> q c t i", i=4, t=4)
+            dst = grouped(key, "by_slot")[:, S * n : S * (n + 1)].rearrange("q (c i t) -> q c t i", i=4, t=4)
             if engine == "s":
                 nc.scalar.copy(out=dst, in_=src)
             else:
                 nc.vector.tensor_copy(out=dst, in_=src)
 
-        def slot_quantize(key, half, g, sb):
-            quantize(g, sb, 2 * P * half, st[key, "sg", half][:])
+        def slot_quantize(key, g, sb, first=0, tiles=4):
+            quantize(g, sb, P * first, st[key, "by_slot"][:, S * first : S * (first + tiles)])
 
         def a_mm(t):
             st["A", "acc", t] = product(PT, A, t, A)
@@ -290,7 +297,12 @@ def tile_mayer_bond_orders_s4_kernel(tc, pt_words, pt_scales, s_words, s_scales,
         def o_store(sb, t, first=0, width=R):
             cols = slice(first, first + width)
             res = work.tile([P, width], F32, name="res", bufs=8)
-            nc.vector.tensor_tensor(out=res[:], in0=st["out", sb, t, first], in1=st["b_row"][:, cols], op=ADD)
+            if (sb, t) in ASIDE:
+                raw = work.tile([P, width], F32, name="raw", bufs=2)
+                nc.scalar.copy(out=raw[:], in_=st["out", sb, t, first])
+                nc.gpsimd.tensor_tensor(out=res[:], in0=raw[:], in1=b_row[:, cols], op=ADD)
+            else:
+                nc.vector.tensor_tensor(out=res[:], in0=st["out", sb, t, first], in1=b_row[:, cols], op=ADD)
             rows = out[S * sb : S * (sb + 1), cols]
             dst = rows[P * t : P * (t + 1), :] if sb == A else rows.rearrange("(p t) r -> t p r", t=4)[t]
             nc.sync.dma_start(out=dst, in_=res[:])
@@ -302,13 +314,9 @@ def tile_mayer_bond_orders_s4_kernel(tc, pt_words, pt_scales, s_words, s_scales,
             st["v_row", A], copy = spread(v_nat, "v_row_a", word_in, word_out, ue)
             copy()
 
-        def spread_vc():
-            st["v_row", C], copy = spread(v_slot[:, 1, :], "v_row_c", "q (u e p) -> q u p e", word_out, ue)
-            copy()
-
-        def spread_b():
-            st["b_row"], copy = spread(b_slot, "b_row", "q (t p) -> q p t", "q (p t) -> q p t", dict(t=4))
-            copy()
+        def sort_vc():
+            st["v_row", C] = keep.tile([P, S], F32, name="v_row_c")
+            nc.scalar.copy(out=as_word(st["v_row", C][:]), in_=by_word(v_c16[:]))
 
         def pair_step(x, y, t):
             p_mm(x, y, t)
@@ -331,13 +339,19 @@ def tile_mayer_bond_orders_s4_kernel(tc, pt_words, pt_scales, s_words, s_scales,
             a_scaled(t)
             if t < 2:
                 a_plain(t)
-        for op, t in ((PT, 0), (PT, 1), (OV, 0), (OV, 1), (PT, 2), (OV, 2), (PT, 3), (OV, 3)):
-            gather_slot(op, B, t)
-        spread_va()
+        for t in range(4):
+            gather_codes(PT, B, t)
+        gather_scales(PT, B, 0)
+        gather_slot(OV, B, 0)
+        gather_slot(OV, B, 1)
+        gather_scales(PT, B, 2)
+        gather_slot(OV, B, 2)
+        gather_slot(OV, B, 3)
         a_plain(2)
         a_plain(3)
         widen()
         pair_step(B, A, 0)
+        spread_va()
         for t in range(4):
             turn("A", "scaled", t)
         p_bond(B, A, 0)
@@ -351,19 +365,18 @@ def tile_mayer_bond_orders_s4_kernel(tc, pt_words, pt_scales, s_words, s_scales,
         pair_step(B, A, 2)
         p_rows(B, A, 1)
         word_both("A")
-        spread_vc()
         p_bond(B, A, 2)
         word_copy("A", 0)
         word_copy("A", 1)
         fill(1)
         pair_step(B, A, 3)
+        sort_vc()
         p_rows(B, A, 2)
-        word_quantize("A", 0, A, A)
-        word_quantize("A", 1, A, A)
+        word_quantize("A", A, A)
         fill(1)
         p_bond(B, A, 3)
 
-        def diag_after_pair(sb, x, y, extra, eng, before):
+        def diag_after_pair(sb, x, y, eng, before):
             k = (x, y)
             d_mm(sb, 0)
             d_copy(sb, 0)
@@ -376,49 +389,42 @@ def tile_mayer_bond_orders_s4_kernel(tc, pt_words, pt_scales, s_words, s_scales,
             fill(1)
             d_mm(sb, 2)
             d_copy(sb, 2)
-            interleave(k, 0, eng)
             fill(1)
             d_mm(sb, 3)
-            word_both(k)
-            extra()
             d_copy(sb, 3)
-            interleave(k, 1, "v")
             fill(1)
-            word_copy(k, 0)
-            word_copy(k, 1)
 
         def pair_after_diag(x, y, sb, px, py, eng, outs=()):
             k = (px, py)
             pair_step(x, y, 0)
-            interleave(k, 2, eng)
-            interleave(k, 3, eng)
-            fill(2)
-            slot_quantize(k, 0, px, py)
-            word_quantize(k, 0, py, px)
+            interleave(k, 0, eng[0])
+            interleave(k, 1, eng[1])
+            fill(1)
+            word_both(k)
             for t in range(4):
                 turn(sb, "plain", t)
+            word_copy(k, 0)
+            word_copy(k, 1)
             p_bond(x, y, 0)
             d_bond(sb, 0)
             d_bond(sb, 1)
-            word_quantize(k, 1, py, px)
             pair_step(x, y, 1)
+            interleave(k, 2, eng[2])
             d_bond(sb, 2)
             d_bond(sb, 3)
             p_bond(x, y, 1)
-            slot_quantize(k, 1, px, py)
+            word_quantize(k, py, px)
             p_rows(x, y, 0)
+            interleave(k, 3, eng[3])
+            pair_step(x, y, 2)
             interleave(sb, 0, "s")
+            p_rows(x, y, 1)
+            p_bond(x, y, 2)
+            slot_quantize(k, px, py)
             for o in outs[:1]:
                 o_mm(*o)
-                interleave(sb, 1, "s")
-            pair_step(x, y, 2)
-            p_rows(x, y, 1)
-            for o in outs[:1]:
                 o_store(*o)
-            if not outs:
-                interleave(sb, 1, "s")
-            p_bond(x, y, 2)
-            interleave(sb, 2, "s")
+            interleave(sb, 1, "s")
             for o in outs[1:2]:
                 o_mm(*o)
                 word_turn((x, y), 0)
@@ -426,20 +432,23 @@ def tile_mayer_bond_orders_s4_kernel(tc, pt_words, pt_scales, s_words, s_scales,
                 o_store(*o)
             pair_step(x, y, 3)
             p_rows(x, y, 2)
-            slot_quantize(sb, 0, sb, sb)
             for o in outs[1:2]:
-                word_quantize((x, y), 0, y, x)
-            interleave(sb, 3, "s")
+                slot_quantize(sb, sb, sb, 0, 2)
+                word_quantize((x, y), y, x, 0, 2)
             p_bond(x, y, 3)
 
-        diag_after_pair(B, B, A, spread_b, "s", lambda: None)
-        pair_after_diag(B, C, B, B, A, "s")
-        diag_after_pair(C, B, C, lambda: None, "v", lambda: slot_quantize(B, 1, B, B))
-        pair_after_diag(C, A, C, B, C, "v", [(B, 0), (B, 1)])
+        def finish_b():
+            interleave(B, 2, "v")
+            interleave(B, 3, "v")
+            slot_quantize(B, B, B)
+
+        diag_after_pair(B, B, A, "ssss", lambda: None)
+        pair_after_diag(B, C, B, B, A, "ssss")
+        diag_after_pair(C, B, C, "vvss", finish_b)
+        pair_after_diag(C, A, C, B, C, "vvss", [(B, 0), (B, 1)])
         k = (C, A)
         p_slot(C, A, 3)
         o_mm(B, 2)
-        slot_quantize(C, 1, C, C)
         p_rows(C, A, 3)
         o_mm(B, 3)
         interleave(k, 0, "s")
@@ -448,18 +457,21 @@ def tile_mayer_bond_orders_s4_kernel(tc, pt_words, pt_scales, s_words, s_scales,
         o_mm(C, 0)
         word_turn(k, 1)
         interleave(k, 2, "s")
-        slot_quantize(k, 0, C, A)
+        slot_quantize(k, C, A, 0, 2)
         o_store(B, 3)
         o_mm(C, 1)
         interleave(k, 3, "s")
         word_copy(k, 1)
+        interleave(C, 2, "s")
+        interleave(C, 3, "s")
         o_store(C, 0)
         o_mm(A, 0)
-        slot_quantize(k, 1, C, A)
+        slot_quantize(k, C, A, 2, 2)
         o_store(C, 1)
         o_mm(A, 1)
-        word_quantize(k, 1, A, C)
+        word_quantize(k, A, C, 2, 2)
         o_store(A, 0)
+        slot_quantize(C, C, C, 2, 2)
         rows = [(A, 1), (A, 2), (A, 3), (C, 2), (C, 3, 0, 256), (C, 3, 256, 256)]
         for n in range(1, 6):
             o_mm(*rows[n])

@@ -18,12 +18,12 @@ ADD = mybir.AluOpType.add
 COPY = mybir.ActivationFunctionType.Copy
 
 P = 128
-G = 3
-S = 512
+BLK = 512
+PASSES = N // BLK
+TILES = BLK // P
+BANKS = 8
 A, B, C = 0, 1, 2
 PT, OV = 0, 1
-BANKS = 8
-ASIDE = ()
 
 
 def tile_mayer_bond_orders_s4_kernel(tc, pt_words, pt_scales, s_words, s_scales, v, w_words, w_scales, b, out):
@@ -37,443 +37,418 @@ def tile_mayer_bond_orders_s4_kernel(tc, pt_words, pt_scales, s_words, s_scales,
         psum = ctx.enter_context(tc.psum_pool(name="psum", bufs=1))
         ctx.enter_context(tc.manual_schedule())
 
-        taken = []
+        handed_out = []
 
         def bank():
-            taken.append(0)
-            return psum.tile([P, S], F32, name="bank%d" % (len(taken) % BANKS))
+            handed_out.append(0)
+            return psum.tile([P, BLK], F32, name="bank%d" % (len(handed_out) % BANKS))
 
         codes, planes = {}, {}
 
-        def load_codes(queue, op, sb):
-            t = keep.tile([P, G, 2 * S], U8, name="codes%d%d" % (op, sb), align_bytes=64)
-            src = words_hbm[op][:, :, 2 * S * sb : 2 * S * (sb + 1)].rearrange("g p c -> p g c")
-            queue.dma_start(out=t[:].bitcast(I32), in_=src.bitcast(I32))
-            codes[op, sb] = t
+        def load_codes(op, blk):
+            tile = keep.tile([P, PASSES, 2 * BLK], U8, name="codes%d%d" % (op, blk), align_bytes=64)
+            src = words_hbm[op][:, :, 2 * BLK * blk : 2 * BLK * (blk + 1)].rearrange("g p c -> p g c")
+            nc.sync.dma_start(out=tile[:].bitcast(I32), in_=src.bitcast(I32))
+            codes[op, blk] = tile
 
         def blank_plane(engine, name, width):
-            t = keep.tile([P, G, width], U8, name=name, align_bytes=64)
-            engine.memset(t[:].bitcast(I32), 0)
-            return t
+            tile = keep.tile([P, PASSES, width], U8, name=name, align_bytes=64)
+            engine.memset(tile[:].bitcast(I32), 0)
+            return tile
 
-        def load_plane(t, hbm, which, queue=nc.sync):
+        def load_plane(plane, hbm, quadrants):
             rows = hbm.rearrange("g (q r) n -> q r g n", r=4)
-            for r in which:
-                queue.dma_start(out=t[32 * r : 32 * r + 4, :, :].bitcast(I32), in_=rows[r].bitcast(I32))
+            for q in quadrants:
+                nc.sync.dma_start(out=plane[32 * q : 32 * q + 4, :, :].bitcast(I32), in_=rows[q].bitcast(I32))
 
-        ident = keep.tile([P, P], F32, name="ident")
-        make_identity(nc, ident[:])
-        late = {}
+        for op, engine in ((PT, nc.gpsimd), (OV, nc.vector)):
+            planes[op, A] = blank_plane(engine, "plane%da" % op, BLK)[:]
+        planes_bc = {}
         for op in (PT, OV):
-            planes[op, A] = blank_plane(nc.vector, "plane%da" % op, S)[:]
-        for op in (PT, OV):
-            late[op] = blank_plane(nc.vector, "plane%dbc" % op, 2 * S)
-            planes[op, B], planes[op, C] = late[op][:, :, :S], late[op][:, :, S:]
+            planes_bc[op] = blank_plane(nc.vector, "plane%dbc" % op, 2 * BLK)
+            planes[op, B], planes[op, C] = planes_bc[op][:, :, :BLK], planes_bc[op][:, :, BLK:]
         w_plane = blank_plane(nc.vector, "w_plane", R)
 
-        v_nat16 = keep.tile([P, 4, 2], BF16, name="v_nat16")
-        v_slot16 = keep.tile([P, 2, 4], BF16, name="v_slot16")
-        v_c16 = keep.tile([P, S], BF16, name="v_c16")
+        v_tile16 = keep.tile([P, TILES, 2], BF16, name="v_tile16")
+        v_slot16 = keep.tile([P, 2, TILES], BF16, name="v_slot16")
+        v_c16 = keep.tile([P, BLK], BF16, name="v_c16")
         b_row = keep.tile([P, R], BF16, name="b_row")
-        w_codes = keep.tile([P, G, 4 * R], U8, name="w_codes", align_bytes=64)
+        w_codes = keep.tile([P, PASSES, 4 * R], U8, name="w_codes", align_bytes=64)
 
         with nc.allow_non_contiguous_dma(reason="one value of v to a partition"):
-            nc.gpsimd.dma_start(out=v_nat16[:, :, 0:1], in_=v[0:S].rearrange("(a p o) -> p a o", p=P, o=1))
-        nc.gpsimd.dma_start(out=v_slot16[:], in_=v[S:N].rearrange("(g p t) -> p g t", p=P, t=4))
-        load_plane(planes[PT, A], pt_scales[:, :, :S], range(3))
-        load_codes(nc.sync, OV, A)
-        load_codes(nc.sync, PT, A)
-        load_plane(planes[PT, A], pt_scales[:, :, :S], range(3, 4))
-        load_plane(planes[OV, A], s_scales[:, :, :S], range(4))
+            nc.gpsimd.dma_start(out=v_tile16[:, :, 0:1], in_=v[:BLK].rearrange("(a p o) -> p a o", p=P, o=1))
+        nc.gpsimd.dma_start(out=v_slot16[:], in_=v[BLK:].rearrange("(g p t) -> p g t", p=P, t=TILES))
+        ident = keep.tile([P, P], F32, name="ident")
+        make_identity(nc, ident[:])
+
+        load_plane(planes[PT, A], pt_scales[:, :, :BLK], range(3))
+        load_codes(OV, A)
+        load_codes(PT, A)
+        load_plane(planes[PT, A], pt_scales[:, :, :BLK], range(3, 4))
+        load_plane(planes[OV, A], s_scales[:, :, :BLK], range(4))
         for op in (PT, OV):
-            load_codes(nc.sync, op, B)
+            load_codes(op, B)
         for op in (PT, OV):
-            load_plane(late[op], scales_hbm[op][:, :, S:], range(4))
-        load_codes(nc.sync, PT, C)
-        load_codes(nc.sync, OV, C)
-        nc.sync.dma_start(out=v_c16[:], in_=v[2 * S :].partition_broadcast(P))
+            load_plane(planes_bc[op], scales_hbm[op][:, :, BLK:], range(4))
+        for op in (PT, OV):
+            load_codes(op, C)
+        nc.sync.dma_start(out=v_c16[:], in_=v[2 * BLK :].partition_broadcast(P))
         load_plane(w_plane, w_scales, range(4))
         nc.sync.dma_start(out=w_codes[:].bitcast(I32), in_=w_words.rearrange("g p n t -> p g (n t)").bitcast(I32))
         nc.sync.dma_start(out=b_row[:], in_=b.partition_broadcast(P))
 
-        v_nat = keep.tile([P, 4], F32, name="v_nat")
-        v_slot = keep.tile([P, 2, 4], F32, name="v_slot")
-        nc.scalar.activation(out=v_nat[:], in_=v_nat16[:, :, 0], func=COPY)
-
-        def widen():
-            nc.scalar.activation(out=v_slot[:], in_=v_slot16[:], func=COPY)
-
-        def v_col(sb, t):
-            return v_slot[:, sb - 1, t : t + 1]
+        v_tile = keep.tile([P, TILES], F32, name="v_tile")
+        v_slot = keep.tile([P, 2, TILES], F32, name="v_slot")
+        nc.scalar.activation(out=v_tile[:], in_=v_tile16[:, :, 0], func=COPY)
 
         slot_codes, slot_planes = {}, {}
 
-        def gather_codes(op, sb, t):
-            c = keep.tile([P, G, 2 * P], U8, name="slot_codes%d%d%d" % (op, sb, t), align_bytes=64)
+        def gather_codes(op, blk, t):
+            tile = keep.tile([P, 2, PASSES, 2 * P], U8, name="slot_codes%d%d%d" % (op, blk, t), align_bytes=64)
             nc.vector.tensor_copy(
-                out=c[:].rearrange("q g (m e) -> q g m e", e=2),
-                in_=codes[op, sb][:].rearrange("q g (m t e) -> q t g m e", t=4, e=2)[:, t],
+                out=tile[:].rearrange("q t g (m e) -> q t g m e", e=2),
+                in_=codes[op, blk][:].rearrange("q g (m t e) -> q t g m e", t=TILES, e=2)[:, t : t + 2],
             )
-            slot_codes[op, sb, t] = c
+            slot_codes[op, blk, t], slot_codes[op, blk, t + 1] = tile[:, 0], tile[:, 1]
 
-        def gather_scales(op, sb, t):
-            s = keep.tile([P, 2, G, P], U8, name="slot_plane%d%d%d" % (op, sb, t), align_bytes=64)
-            nc.vector.tensor_copy(out=s[:], in_=planes[op, sb].rearrange("q g (m t) -> q t g m", t=4)[:, t : t + 2])
-            slot_planes[op, sb, t], slot_planes[op, sb, t + 1] = s[:, 0], s[:, 1]
+        def gather_scales(op, blk, t):
+            tile = keep.tile([P, 2, PASSES, P], U8, name="slot_plane%d%d%d" % (op, blk, t), align_bytes=64)
+            nc.vector.tensor_copy(out=tile[:], in_=planes[op, blk].rearrange("q g (m t) -> q t g m", t=TILES)[:, t : t + 2])
+            slot_planes[op, blk, t], slot_planes[op, blk, t + 1] = tile[:, 0], tile[:, 1]
 
-        def gather_slot(op, sb, t):
-            gather_codes(op, sb, t)
-            if t % 2 == 0:
-                gather_scales(op, sb, t)
+        pending = [(gather, op, t) for op in (PT, OV) for t in (0, 2) for gather in (gather_codes, gather_scales)]
 
-        def product(op, sb, t, moving_sb):
+        def gather_next_of_c():
+            if pending:
+                gather, op, t = pending.pop(0)
+                gather(op, C, t)
+
+        made = {}
+        v_row = {}
+        d_codes, d_planes = {}, {}
+        for partner in (A, B, C):
+            for rows in (A, B, C):
+                d_codes[partner, rows] = keep.tile([P, BLK], U32, name="dq%d%d" % (partner, rows), align_bytes=64)
+                d_planes[partner, rows] = keep.tile([P, BLK], U8, name="dqs%d%d" % (partner, rows), align_bytes=64)
+
+        def to_word_order(ap):
+            return ap.rearrange("q (p u e) -> q u p e", u=2, e=2)
+
+        def in_word_order(ap):
+            return ap.rearrange("q (u p e) -> q u p e", u=2, e=2)
+
+        def product(op, x, y, t):
             acc = bank()
-            for g in range(G):
-                if sb == A:
-                    lhs = codes[op, sb][:, g, 2 * P * t : 2 * P * (t + 1)]
-                    lhs_scale = planes[op, sb][:, g, P * t : P * (t + 1)]
+            for g in range(PASSES):
+                if x == A:
+                    lhs = codes[op, x][:, g, 2 * P * t : 2 * P * (t + 1)]
+                    lhs_scale = planes[op, x][:, g, P * t : P * (t + 1)]
                 else:
-                    lhs = slot_codes[op, sb, t][:, g, :]
-                    lhs_scale = slot_planes[op, sb, t][:, g, :]
+                    lhs = slot_codes[op, x, t][:, g, :]
+                    lhs_scale = slot_planes[op, x, t][:, g, :]
                 nc.tensor.matmul_mx(
                     out=acc[:],
                     lhsT=lhs.bitcast(FP4X4),
                     lhsT_scale=lhs_scale,
-                    rhs=codes[1 - op, moving_sb][:, g, :].bitcast(FP4X4),
-                    rhs_scale=planes[1 - op, moving_sb][:, g, :],
+                    rhs=codes[1 - op, y][:, g, :].bitcast(FP4X4),
+                    rhs_scale=planes[1 - op, y][:, g, :],
                     start=(g == 0),
-                    stop=(g == G - 1),
+                    stop=(g == PASSES - 1),
                 )
-            return acc
+            made[(x, y), op, t] = acc
 
-        def by_word(ap):
-            return ap.rearrange("q (p u e) -> q u p e", u=2, e=2)
-
-        def as_word(ap):
-            return ap.rearrange("q (u p e) -> q u p e", u=2, e=2)
-
-        def spread(cols, name, pattern_in, pattern_out, sizes):
+        def mirror(x, t):
             acc = bank()
-            for n in range(4):
-                nc.tensor.transpose(acc[:, P * n : P * (n + 1)], cols[:, n : n + 1].to_broadcast([P, P]), ident[:])
-            t = keep.tile([P, S], F32, name=name)
-            return t, lambda: nc.scalar.copy(out=t[:].rearrange(pattern_out, **sizes), in_=acc[:].rearrange(pattern_in, **sizes))
+            for n in range(TILES):
+                nc.tensor.transpose(acc[:, P * n : P * (n + 1)], made[(x, x), "source", n][:, P * t : P * (t + 1)], ident[:])
+            made[(x, x), "mirror", t] = acc
 
-        d_codes, d_planes = {}, {}
-        for g in range(G):
-            for sb in range(G):
-                d_codes[g, sb] = keep.tile([P, S], U32, name="dq%d%d" % (g, sb), align_bytes=64)
-                d_planes[g, sb] = keep.tile([P, S], U8, name="dqs%d%d" % (g, sb), align_bytes=64)
+        def a_scaled_copy(t):
+            tile = work.tile([P, BLK], F32, name="source", bufs=TILES)
+            nc.scalar.activation(out=tile[:], in_=made[(A, A), PT, t][:], func=COPY, scale=v_tile[:, t : t + 1])
+            made[(A, A), "source", t] = tile
 
-        def quantize(g, sb, first, grouped):
-            n = grouped.shape[1] // 4
-            nc.vector.quantize_mx(
-                out=d_codes[g, sb][:, first : first + n].bitcast(FP8X4),
-                scales=d_planes[g, sb][:, first : first + n],
-                in_=grouped,
+        def copy_in_word_order(x, y, t):
+            name, bufs = ("a_factor", TILES) if y == x else ("factor", 3)
+            tile = work.tile([P, BLK], F32, name=name, bufs=bufs)
+            nc.scalar.copy(out=in_word_order(tile[:]), in_=to_word_order(made[(x, y), PT, t][:]))
+            made[(x, y), "factor", t] = tile
+
+        def rows_tile(pair, t):
+            made[pair, "rows", t] = work.tile([P, BLK], BF16, name="rows", bufs=2 * TILES)
+            return made[pair, "rows", t]
+
+        def a_rows(t):
+            nc.vector.tensor_tensor(
+                out=in_word_order(rows_tile((A, A), t)[:]),
+                in0=to_word_order(made[(A, A), "mirror", t][:]),
+                in1=in_word_order(made[(A, A), "factor", t][:]),
+                op=MULT,
             )
 
-        st = {}
+        def copy_in_slot_order(x, t):
+            tile = work.tile([P, BLK], F32, name="source", bufs=TILES)
+            nc.scalar.copy(
+                out=tile[:].rearrange("q (t p) -> q t p", t=TILES),
+                in_=made[(x, x), PT, t][:].rearrange("q (p t) -> q t p", t=TILES),
+            )
+            made[(x, x), "source", t] = tile
 
-        def word_turn(key, half):
+        def slots_tile(pair):
+            if (pair, "slots") not in made:
+                made[pair, "slots"] = work.tile([P, TILES, BLK], BF16, name="slots", bufs=3)
+            return made[pair, "slots"]
+
+        def self_slot(x, t):
+            nc.vector.scalar_tensor_tensor(
+                out=slots_tile((x, x))[:, t, :],
+                in0=made[(x, x), "mirror", t][:],
+                scalar=v_slot[:, x - 1, t : t + 1],
+                in1=made[(x, x), "source", t][:],
+                op0=MULT,
+                op1=MULT,
+            )
+
+        def bond(x, y, t):
+            tile = work.tile([P, BLK], F32, name="bond", bufs=TILES)
+            nc.vector.tensor_tensor(
+                out=in_word_order(tile[:]),
+                in0=to_word_order(made[(x, y), OV, t][:]),
+                in1=in_word_order(made[(x, y), "factor", t][:]),
+                op=MULT,
+            )
+            made[(x, y), "bond", t] = tile
+
+        def pair_rows(x, y, t):
+            nc.vector.tensor_tensor(out=rows_tile((x, y), t)[:], in0=made[(x, y), "bond", t][:], in1=v_row[y][:], op=MULT)
+
+        def pair_slot(x, y, t):
+            order = "p u e" if y == A else "u e p"
+            nc.scalar.activation(
+                out=slots_tile((x, y))[:, t, :].rearrange("q (%s) -> q %s" % (order, order), u=2, e=2),
+                in_=made[(x, y), "bond", t][:].rearrange("q (u p e) -> q %s" % order, u=2, e=2),
+                func=COPY,
+                scale=v_slot[:, x - 1, t : t + 1],
+            )
+
+        def turn(pair, half):
             acc = bank()
             for n in range(2):
-                words = st[key, "rows", 2 * half + n][:].bitcast(F32)
+                words = made[pair, "rows", 2 * half + n][:].bitcast(F32)
                 for u in range(2):
                     nc.tensor.transpose(acc[:, P * (2 * n + u) : P * (2 * n + u + 1)], words[:, P * u : P * (u + 1)], ident[:])
-            st[key, "turned", half] = acc
+            made[pair, "turned", half] = acc
 
-        def grouped(key, kind):
-            if (key, kind) not in st:
-                st[key, kind] = work.tile([P, 4 * S], BF16, name=kind, bufs=3, align_bytes=64)
-            return st[key, kind]
+        def packed(pair, kind):
+            if (pair, kind) not in made:
+                made[pair, kind] = work.tile([P, TILES * BLK], BF16, name=kind, bufs=3, align_bytes=64)
+            return made[pair, kind]
 
-        def word_copy(key, half):
+        def pack_turned(pair, half):
             nc.scalar.copy(
-                out=grouped(key, "by_word")[:, 2 * S * half : 2 * S * (half + 1)].bitcast(F32).rearrange("q (n r u) -> q n r u", n=2, u=2),
-                in_=st[key, "turned", half][:].rearrange("q (n u r) -> q n r u", n=2, u=2),
+                out=packed(pair, "from_rows")[:, 2 * BLK * half : 2 * BLK * (half + 1)].bitcast(F32).rearrange("q (n r u) -> q n r u", n=2, u=2),
+                in_=made[pair, "turned", half][:].rearrange("q (n u r) -> q n r u", n=2, u=2),
             )
 
-        def word_quantize(key, g, sb, first=0, tiles=4):
-            quantize(g, sb, P * first, st[key, "by_word"][:, S * first : S * (first + tiles)])
-
-        def slots_tile(key):
-            if (key, "slots") not in st:
-                st[key, "slots"] = work.tile([P, 4, S], BF16, name="slots", bufs=3)
-            return st[key, "slots"]
-
-        def interleave(key, n, engine):
-            src = st[key, "slots"][:, :, P * n : P * (n + 1)].rearrange("q t (c i) -> q c t i", i=4)
-            dst = grouped(key, "by_slot")[:, S * n : S * (n + 1)].rearrange("q (c i t) -> q c t i", i=4, t=4)
-            if engine == "s":
-                nc.scalar.copy(out=dst, in_=src)
-            else:
-                nc.vector.tensor_copy(out=dst, in_=src)
-
-        def slot_quantize(key, g, sb, first=0, tiles=4):
-            quantize(g, sb, P * first, st[key, "by_slot"][:, S * first : S * (first + tiles)])
-
-        def a_mm(t):
-            st["A", "acc", t] = product(PT, A, t, A)
-
-        def a_scaled(t):
-            x = work.tile([P, S], F32, name="diag_t", bufs=4)
-            nc.scalar.activation(out=x[:], in_=st["A", "acc", t][:], func=COPY, scale=v_nat[:, t : t + 1])
-            st["A", "scaled", t] = x
-
-        def a_plain(t):
-            x = work.tile([P, S], F32, name="a_plain", bufs=4)
-            nc.scalar.copy(out=as_word(x[:]), in_=by_word(st["A", "acc", t][:]))
-            st["A", "plain", t] = x
-
-        def turn(key, name, t):
-            acc = bank()
-            for n in range(4):
-                nc.tensor.transpose(acc[:, P * n : P * (n + 1)], st[key, name, n][:, P * t : P * (t + 1)], ident[:])
-            st[key, "mirror", t] = acc
-
-        def a_bond(t):
-            x = work.tile([P, S], BF16, name="rows", bufs=8)
-            nc.vector.tensor_tensor(out=as_word(x[:]), in0=by_word(st["A", "mirror", t][:]), in1=as_word(st["A", "plain", t][:]), op=MULT)
-            st["A", "rows", t] = x
-
-        def d_mm(sb, t):
-            st[sb, "acc", t] = product(PT, sb, t, sb)
-
-        def d_copy(sb, t):
-            x = work.tile([P, S], F32, name="diag_t", bufs=4)
-            nc.scalar.copy(out=x[:].rearrange("q (t p) -> q t p", t=4), in_=st[sb, "acc", t][:].rearrange("q (p t) -> q t p", t=4))
-            st[sb, "plain", t] = x
-
-        def d_bond(sb, t):
-            nc.vector.scalar_tensor_tensor(
-                out=slots_tile(sb)[:, t, :], in0=st[sb, "mirror", t][:], scalar=v_col(sb, t), in1=st[sb, "plain", t][:], op0=MULT, op1=MULT
+        def pack_slots(pair, n, copy):
+            copy(
+                out=packed(pair, "from_slots")[:, BLK * n : BLK * (n + 1)].rearrange("q (c i t) -> q c t i", i=4, t=TILES),
+                in_=made[pair, "slots"][:, :, P * n : P * (n + 1)].rearrange("q t (c i) -> q c t i", i=4),
             )
 
-        def p_mm(x, y, t):
-            st[(x, y), "p", t] = product(PT, x, t, y)
-            st[(x, y), "q", t] = product(OV, x, t, y)
-
-        def p_copy(x, y, t):
-            z = work.tile([P, S], F32, name="pair_t", bufs=3)
-            nc.scalar.copy(out=as_word(z[:]), in_=by_word(st[(x, y), "p", t][:]))
-            st[(x, y), "plain", t] = z
-
-        def p_bond(x, y, t):
-            z = work.tile([P, S], F32, name="bond", bufs=4)
-            nc.vector.tensor_tensor(out=as_word(z[:]), in0=by_word(st[(x, y), "q", t][:]), in1=as_word(st[(x, y), "plain", t][:]), op=MULT)
-            st[(x, y), "bond", t] = z
-
-        def p_rows(x, y, t):
-            z = work.tile([P, S], BF16, name="rows", bufs=8)
-            nc.vector.tensor_tensor(out=z[:], in0=st[(x, y), "bond", t][:], in1=st["v_row", y][:], op=MULT)
-            st[(x, y), "rows", t] = z
-
-        def p_slot(x, y, t):
-            order = "p u e" if y == A else "u e p"
-            sizes = dict(u=2, e=2)
-            nc.scalar.activation(
-                out=slots_tile((x, y))[:, t, :].rearrange("q (%s) -> q %s" % (order, order), **sizes),
-                in_=st[(x, y), "bond", t][:].rearrange("q (u p e) -> q %s" % order, **sizes),
-                func=COPY,
-                scale=v_col(x, t),
+        def quantize(pair, kind, first=0, tiles=TILES):
+            x, y = pair
+            key = (y, x) if kind == "from_rows" else (x, y)
+            cols = slice(P * first, P * (first + tiles))
+            nc.vector.quantize_mx(
+                out=d_codes[key][:, cols].bitcast(FP8X4),
+                scales=d_planes[key][:, cols],
+                in_=made[pair, kind][:, BLK * first : BLK * (first + tiles)],
             )
 
-        def o_mm(sb, t, first=0, width=R):
+        def out_matmul(blk, t, first=0, width=R):
             acc = bank()[:][:, :width]
             cols = slice(first, first + width)
-            for g in range(G):
+            for g in range(PASSES):
                 nc.tensor.matmul_mx(
                     out=acc,
-                    lhsT=d_codes[g, sb][:, P * t : P * (t + 1)].bitcast(FP8X4),
-                    lhsT_scale=d_planes[g, sb][:, P * t : P * (t + 1)],
+                    lhsT=d_codes[g, blk][:, P * t : P * (t + 1)].bitcast(FP8X4),
+                    lhsT_scale=d_planes[g, blk][:, P * t : P * (t + 1)],
                     rhs=w_codes[:, g, :].bitcast(FP8X4)[:, cols],
                     rhs_scale=w_plane[:, g, cols],
                     start=(g == 0),
-                    stop=(g == G - 1),
+                    stop=(g == PASSES - 1),
                 )
-            st["out", sb, t, first] = acc
+            made["out", blk, t, first] = acc
 
-        def o_store(sb, t, first=0, width=R):
+        def out_store(blk, t, first=0, width=R):
             cols = slice(first, first + width)
             res = work.tile([P, width], F32, name="res", bufs=8)
-            if (sb, t) in ASIDE:
-                raw = work.tile([P, width], F32, name="raw", bufs=2)
-                nc.scalar.copy(out=raw[:], in_=st["out", sb, t, first])
-                nc.gpsimd.tensor_tensor(out=res[:], in0=raw[:], in1=b_row[:, cols], op=ADD)
-            else:
-                nc.vector.tensor_tensor(out=res[:], in0=st["out", sb, t, first], in1=b_row[:, cols], op=ADD)
-            rows = out[S * sb : S * (sb + 1), cols]
-            dst = rows[P * t : P * (t + 1), :] if sb == A else rows.rearrange("(p t) r -> t p r", t=4)[t]
+            nc.vector.tensor_tensor(out=res[:], in0=made["out", blk, t, first], in1=b_row[:, cols], op=ADD)
+            rows = out[BLK * blk : BLK * (blk + 1), cols]
+            dst = rows[P * t : P * (t + 1), :] if blk == A else rows.rearrange("(p t) r -> t p r", t=TILES)[t]
             nc.sync.dma_start(out=dst, in_=res[:])
 
-
-        word_in, word_out, ue = "q (p u e) -> q u p e", "q (u p e) -> q u p e", dict(u=2, e=2)
-
-        def spread_va():
-            st["v_row", A], copy = spread(v_nat, "v_row_a", word_in, word_out, ue)
-            copy()
-
-        def sort_vc():
-            st["v_row", C] = keep.tile([P, S], F32, name="v_row_c")
-            nc.scalar.copy(out=as_word(st["v_row", C][:]), in_=by_word(v_c16[:]))
-
         def pair_step(x, y, t):
-            p_mm(x, y, t)
-            p_copy(x, y, t)
+            product(PT, x, y, t)
+            product(OV, x, y, t)
+            copy_in_word_order(x, y, t)
             if t > 0:
-                p_slot(x, y, t - 1)
+                pair_slot(x, y, t - 1)
 
-        def word_both(key):
-            word_turn(key, 0)
-            word_turn(key, 1)
+        on_scalar, on_vector = nc.scalar.copy, nc.vector.tensor_copy
 
-        todo = [(PT, C, t) for t in range(4)] + [(OV, C, t) for t in range(4)]
 
-        def fill(count):
-            for i in range(min(count, len(todo))):
-                gather_slot(*todo.pop(0))
-
-        for t in range(4):
-            a_mm(t)
-            a_scaled(t)
-            if t < 2:
-                a_plain(t)
-        for t in range(4):
-            gather_codes(PT, B, t)
+        aa, ba, bb, bc, cc, ca = (A, A), (B, A), (B, B), (B, C), (C, C), (C, A)
+        for t in range(TILES):
+            product(PT, A, A, t)
+            a_scaled_copy(t)
+            if t == 0:
+                copy_in_word_order(A, A, t)
+        gather_codes(PT, B, 0)
+        gather_codes(OV, B, 0)
         gather_scales(PT, B, 0)
-        gather_slot(OV, B, 0)
-        gather_slot(OV, B, 1)
+        gather_codes(PT, B, 2)
+        gather_scales(OV, B, 0)
+        gather_codes(OV, B, 2)
         gather_scales(PT, B, 2)
-        gather_slot(OV, B, 2)
-        gather_slot(OV, B, 3)
-        a_plain(2)
-        a_plain(3)
-        widen()
-        pair_step(B, A, 0)
-        spread_va()
-        for t in range(4):
-            turn("A", "scaled", t)
-        p_bond(B, A, 0)
-        a_bond(0)
-        a_bond(1)
+        gather_scales(OV, B, 2)
+
+        product(PT, B, A, 0)
+        for t in range(1, TILES):
+            copy_in_word_order(A, A, t)
+        nc.scalar.activation(out=v_slot[:], in_=v_slot16[:], func=COPY)
+        copy_in_word_order(B, A, 0)
+        spread = bank()
+        for t in range(TILES):
+            nc.tensor.transpose(spread[:, P * t : P * (t + 1)], v_tile[:, t : t + 1].to_broadcast([P, P]), ident[:])
+        v_row[A] = keep.tile([P, BLK], F32, name="v_row_a")
+        nc.scalar.copy(out=in_word_order(v_row[A][:]), in_=to_word_order(spread[:]))
+        for t in range(TILES):
+            mirror(A, t)
+        a_rows(0)
+        product(OV, B, A, 0)
+        a_rows(1)
+        bond(B, A, 0)
         pair_step(B, A, 1)
-        a_bond(2)
-        a_bond(3)
-        p_bond(B, A, 1)
-        p_rows(B, A, 0)
+        a_rows(2)
+        a_rows(3)
+        bond(B, A, 1)
+        pair_rows(B, A, 0)
         pair_step(B, A, 2)
-        p_rows(B, A, 1)
-        word_both("A")
-        p_bond(B, A, 2)
-        word_copy("A", 0)
-        word_copy("A", 1)
-        fill(1)
+        pair_rows(B, A, 1)
+        turn(aa, 0)
+        turn(aa, 1)
+        bond(B, A, 2)
+        pack_turned(aa, 0)
+        pack_turned(aa, 1)
+        gather_next_of_c()
         pair_step(B, A, 3)
-        sort_vc()
-        p_rows(B, A, 2)
-        word_quantize("A", A, A)
-        fill(1)
-        p_bond(B, A, 3)
+        v_row[C] = keep.tile([P, BLK], F32, name="v_row_c")
+        nc.scalar.copy(out=in_word_order(v_row[C][:]), in_=to_word_order(v_c16[:]))
+        pair_rows(B, A, 2)
+        quantize(aa, "from_rows")
+        gather_next_of_c()
+        bond(B, A, 3)
 
-        def diag_after_pair(sb, x, y, eng, before):
-            k = (x, y)
-            d_mm(sb, 0)
-            d_copy(sb, 0)
-            p_slot(x, y, 3)
-            fill(1)
-            p_rows(x, y, 3)
-            d_mm(sb, 1)
-            d_copy(sb, 1)
-            before()
-            fill(1)
-            d_mm(sb, 2)
-            d_copy(sb, 2)
-            fill(1)
-            d_mm(sb, 3)
-            d_copy(sb, 3)
-            fill(1)
+        def self_step(x, t):
+            product(PT, x, x, t)
+            copy_in_slot_order(x, t)
 
-        def pair_after_diag(x, y, sb, px, py, eng, outs=()):
-            k = (px, py)
+        def first_steps(x, y, last, own, early_pack):
             pair_step(x, y, 0)
-            interleave(k, 0, eng[0])
-            interleave(k, 1, eng[1])
-            fill(1)
-            word_both(k)
-            for t in range(4):
-                turn(sb, "plain", t)
-            word_copy(k, 0)
-            word_copy(k, 1)
-            p_bond(x, y, 0)
-            d_bond(sb, 0)
-            d_bond(sb, 1)
+            pack_slots(last, 0, early_pack)
+            pack_slots(last, 1, early_pack)
+            gather_next_of_c()
+            turn(last, 0)
+            turn(last, 1)
+            for t in range(TILES):
+                mirror(own, t)
+            pack_turned(last, 0)
+            pack_turned(last, 1)
+            bond(x, y, 0)
+            self_slot(own, 0)
+            self_slot(own, 1)
             pair_step(x, y, 1)
-            interleave(k, 2, eng[2])
-            d_bond(sb, 2)
-            d_bond(sb, 3)
-            p_bond(x, y, 1)
-            word_quantize(k, py, px)
-            p_rows(x, y, 0)
-            interleave(k, 3, eng[3])
+            pack_slots(last, 2, on_scalar)
+            self_slot(own, 2)
+            self_slot(own, 3)
+            bond(x, y, 1)
+            quantize(last, "from_rows")
+            pair_rows(x, y, 0)
+            pack_slots(last, 3, on_scalar)
             pair_step(x, y, 2)
-            interleave(sb, 0, "s")
-            p_rows(x, y, 1)
-            p_bond(x, y, 2)
-            slot_quantize(k, px, py)
-            for o in outs[:1]:
-                o_mm(*o)
-                o_store(*o)
-            interleave(sb, 1, "s")
-            for o in outs[1:2]:
-                o_mm(*o)
-                word_turn((x, y), 0)
-                word_copy((x, y), 0)
-                o_store(*o)
-            pair_step(x, y, 3)
-            p_rows(x, y, 2)
-            for o in outs[1:2]:
-                slot_quantize(sb, sb, sb, 0, 2)
-                word_quantize((x, y), y, x, 0, 2)
-            p_bond(x, y, 3)
+            pack_slots((own, own), 0, on_scalar)
+            pair_rows(x, y, 1)
+            bond(x, y, 2)
+            quantize(last, "from_slots")
 
-        def finish_b():
-            interleave(B, 2, "v")
-            interleave(B, 3, "v")
-            slot_quantize(B, B, B)
+        for t in range(TILES):
+            self_step(B, t)
+            if t == 0:
+                pair_slot(B, A, 3)
+            gather_next_of_c()
+            if t == 0:
+                pair_rows(B, A, 3)
 
-        diag_after_pair(B, B, A, "ssss", lambda: None)
-        pair_after_diag(B, C, B, B, A, "ssss")
-        diag_after_pair(C, B, C, "vvss", finish_b)
-        pair_after_diag(C, A, C, B, C, "vvss", [(B, 0), (B, 1)])
-        k = (C, A)
-        p_slot(C, A, 3)
-        o_mm(B, 2)
-        p_rows(C, A, 3)
-        o_mm(B, 3)
-        interleave(k, 0, "s")
-        interleave(k, 1, "v")
-        o_store(B, 2)
-        o_mm(C, 0)
-        word_turn(k, 1)
-        interleave(k, 2, "s")
-        slot_quantize(k, C, A, 0, 2)
-        o_store(B, 3)
-        o_mm(C, 1)
-        interleave(k, 3, "s")
-        word_copy(k, 1)
-        interleave(C, 2, "s")
-        interleave(C, 3, "s")
-        o_store(C, 0)
-        o_mm(A, 0)
-        slot_quantize(k, C, A, 2, 2)
-        o_store(C, 1)
-        o_mm(A, 1)
-        word_quantize(k, A, C, 2, 2)
-        o_store(A, 0)
-        slot_quantize(C, C, C, 2, 2)
-        rows = [(A, 1), (A, 2), (A, 3), (C, 2), (C, 3, 0, 256), (C, 3, 256, 256)]
-        for n in range(1, 6):
-            o_mm(*rows[n])
-            o_store(*rows[n - 1])
-        o_store(*rows[-1])
+        first_steps(B, C, ba, B, on_scalar)
+        pack_slots(bb, 1, on_scalar)
+        pair_step(B, C, 3)
+        pair_rows(B, C, 2)
+        bond(B, C, 3)
+
+        self_step(C, 0)
+        pair_slot(B, C, 3)
+        gather_next_of_c()
+        pair_rows(B, C, 3)
+        self_step(C, 1)
+        pack_slots(bb, 2, on_vector)
+        pack_slots(bb, 3, on_vector)
+        quantize(bb, "from_slots")
+        self_step(C, 2)
+        self_step(C, 3)
+
+        first_steps(C, A, bc, C, on_vector)
+        out_matmul(B, 0)
+        out_store(B, 0)
+        pack_slots(cc, 1, on_scalar)
+        out_matmul(B, 1)
+        turn(ca, 0)
+        pack_turned(ca, 0)
+        out_store(B, 1)
+        pair_step(C, A, 3)
+        pair_rows(C, A, 2)
+        quantize(cc, "from_slots", 0, 2)
+        quantize(ca, "from_rows", 0, 2)
+        bond(C, A, 3)
+
+        pair_slot(C, A, 3)
+        out_matmul(B, 2)
+        pair_rows(C, A, 3)
+        out_matmul(B, 3)
+        pack_slots(ca, 0, on_scalar)
+        pack_slots(ca, 1, on_vector)
+        out_store(B, 2)
+        out_matmul(C, 0)
+        turn(ca, 1)
+        pack_slots(ca, 2, on_scalar)
+        quantize(ca, "from_slots", 0, 2)
+        out_store(B, 3)
+        out_matmul(C, 1)
+        pack_slots(ca, 3, on_scalar)
+        pack_turned(ca, 1)
+        pack_slots(cc, 2, on_scalar)
+        pack_slots(cc, 3, on_scalar)
+        out_store(C, 0)
+        out_matmul(A, 0)
+        quantize(ca, "from_slots", 2, 2)
+        out_store(C, 1)
+        out_matmul(A, 1)
+        quantize(ca, "from_rows", 2, 2)
+        out_store(A, 0)
+        quantize(cc, "from_slots", 2, 2)
+        rest = [(A, 1), (A, 2), (A, 3), (C, 2), (C, 3, 0, R // 2), (C, 3, R // 2, R // 2)]
+        for n in range(1, len(rest)):
+            out_matmul(*rest[n])
+            out_store(*rest[n - 1])
+        out_store(*rest[-1])

from contextlib import ExitStack

import concourse.mybir as mybir
from concourse.masks import make_identity

N, R = 1536, 512
FLOPS = 2 * N * N * N + 2 * N * N * R

F32 = mybir.dt.float32
BF16 = mybir.dt.bfloat16
I32 = mybir.dt.int32
U32 = mybir.dt.uint32
U8 = mybir.dt.uint8
FP4X4 = mybir.dt.float4_e2m1fn_x4
FP8X4 = mybir.dt.float8_e4m3fn_x4
MULT = mybir.AluOpType.mult
ADD = mybir.AluOpType.add
COPY = mybir.ActivationFunctionType.Copy

P = 128
BLK = 512
PASSES = N // BLK
TILES = BLK // P
BANKS = 8
A, B, C = 0, 1, 2
PT, OV = 0, 1


def tile_mayer_bond_orders_s4_kernel(tc, pt_words, pt_scales, s_words, s_scales, v, w_words, w_scales, b, out):
    nc = tc.nc
    words_hbm = (pt_words, s_words)
    scales_hbm = (pt_scales, s_scales)

    with ExitStack() as ctx:
        keep = ctx.enter_context(tc.tile_pool(name="keep", bufs=1))
        work = ctx.enter_context(tc.tile_pool(name="work", bufs=1))
        psum = ctx.enter_context(tc.psum_pool(name="psum", bufs=1))
        ctx.enter_context(tc.manual_schedule())

        handed_out = []

        def bank():
            handed_out.append(0)
            return psum.tile([P, BLK], F32, name="bank%d" % (len(handed_out) % BANKS))

        codes, planes = {}, {}

        def load_codes(op, blk):
            tile = keep.tile([P, PASSES, 2 * BLK], U8, name="codes%d%d" % (op, blk), align_bytes=64)
            src = words_hbm[op][:, :, 2 * BLK * blk : 2 * BLK * (blk + 1)].rearrange("g p c -> p g c")
            nc.sync.dma_start(out=tile[:].bitcast(I32), in_=src.bitcast(I32))
            codes[op, blk] = tile

        def blank_plane(engine, name, width):
            tile = keep.tile([P, PASSES, width], U8, name=name, align_bytes=64)
            engine.memset(tile[:].bitcast(I32), 0)
            return tile

        def load_plane(plane, hbm, quadrants):
            rows = hbm.rearrange("g (q r) n -> q r g n", r=4)
            for q in quadrants:
                nc.sync.dma_start(out=plane[32 * q : 32 * q + 4, :, :].bitcast(I32), in_=rows[q].bitcast(I32))

        for op, engine in ((PT, nc.gpsimd), (OV, nc.vector)):
            planes[op, A] = blank_plane(engine, "plane%da" % op, BLK)[:]
        planes_bc = {}
        for op in (PT, OV):
            planes_bc[op] = blank_plane(nc.vector, "plane%dbc" % op, 2 * BLK)
            planes[op, B], planes[op, C] = planes_bc[op][:, :, :BLK], planes_bc[op][:, :, BLK:]
        w_plane = blank_plane(nc.vector, "w_plane", R)

        v_tile16 = keep.tile([P, TILES, 2], BF16, name="v_tile16")
        v_slot16 = keep.tile([P, 2, TILES], BF16, name="v_slot16")
        v_c16 = keep.tile([P, BLK], BF16, name="v_c16")
        b_row = keep.tile([P, R], BF16, name="b_row")
        w_codes = keep.tile([P, PASSES, 4 * R], U8, name="w_codes", align_bytes=64)

        with nc.allow_non_contiguous_dma(reason="one value of v to a partition"):
            nc.gpsimd.dma_start(out=v_tile16[:, :, 0:1], in_=v[:BLK].rearrange("(a p o) -> p a o", p=P, o=1))
        nc.gpsimd.dma_start(out=v_slot16[:], in_=v[BLK:].rearrange("(g p t) -> p g t", p=P, t=TILES))
        ident = keep.tile([P, P], F32, name="ident")
        make_identity(nc, ident[:])

        load_plane(planes[PT, A], pt_scales[:, :, :BLK], range(3))
        load_codes(OV, A)
        load_codes(PT, A)
        load_plane(planes[PT, A], pt_scales[:, :, :BLK], range(3, 4))
        load_plane(planes[OV, A], s_scales[:, :, :BLK], range(4))
        for op in (PT, OV):
            load_codes(op, B)
        for op in (PT, OV):
            load_plane(planes_bc[op], scales_hbm[op][:, :, BLK:], range(4))
        for op in (PT, OV):
            load_codes(op, C)
        nc.sync.dma_start(out=v_c16[:], in_=v[2 * BLK :].partition_broadcast(P))
        load_plane(w_plane, w_scales, range(4))
        nc.sync.dma_start(out=w_codes[:].bitcast(I32), in_=w_words.rearrange("g p n t -> p g (n t)").bitcast(I32))
        nc.sync.dma_start(out=b_row[:], in_=b.partition_broadcast(P))

        v_tile = keep.tile([P, TILES], F32, name="v_tile")
        v_slot = keep.tile([P, 2, TILES], F32, name="v_slot")
        nc.scalar.activation(out=v_tile[:], in_=v_tile16[:, :, 0], func=COPY)

        slot_codes, slot_planes = {}, {}

        def gather_codes(op, blk, t):
            tile = keep.tile([P, 2, PASSES, 2 * P], U8, name="slot_codes%d%d%d" % (op, blk, t), align_bytes=64)
            nc.vector.tensor_copy(
                out=tile[:].rearrange("q t g (m e) -> q t g m e", e=2),
                in_=codes[op, blk][:].rearrange("q g (m t e) -> q t g m e", t=TILES, e=2)[:, t : t + 2],
            )
            slot_codes[op, blk, t], slot_codes[op, blk, t + 1] = tile[:, 0], tile[:, 1]

        def gather_scales(op, blk, t):
            tile = keep.tile([P, 2, PASSES, P], U8, name="slot_plane%d%d%d" % (op, blk, t), align_bytes=64)
            nc.vector.tensor_copy(out=tile[:], in_=planes[op, blk].rearrange("q g (m t) -> q t g m", t=TILES)[:, t : t + 2])
            slot_planes[op, blk, t], slot_planes[op, blk, t + 1] = tile[:, 0], tile[:, 1]

        pending = [(gather, op, t) for op in (PT, OV) for t in (0, 2) for gather in (gather_codes, gather_scales)]

        def gather_next_of_c():
            if pending:
                gather, op, t = pending.pop(0)
                gather(op, C, t)

        made = {}
        v_row = {}
        d_codes, d_planes = {}, {}
        for partner in (A, B, C):
            for rows in (A, B, C):
                d_codes[partner, rows] = keep.tile([P, BLK], U32, name="dq%d%d" % (partner, rows), align_bytes=64)
                d_planes[partner, rows] = keep.tile([P, BLK], U8, name="dqs%d%d" % (partner, rows), align_bytes=64)

        def to_word_order(ap):
            return ap.rearrange("q (p u e) -> q u p e", u=2, e=2)

        def in_word_order(ap):
            return ap.rearrange("q (u p e) -> q u p e", u=2, e=2)

        def product(op, x, y, t):
            acc = bank()
            for g in range(PASSES):
                if x == A:
                    lhs = codes[op, x][:, g, 2 * P * t : 2 * P * (t + 1)]
                    lhs_scale = planes[op, x][:, g, P * t : P * (t + 1)]
                else:
                    lhs = slot_codes[op, x, t][:, g, :]
                    lhs_scale = slot_planes[op, x, t][:, g, :]
                nc.tensor.matmul_mx(
                    out=acc[:],
                    lhsT=lhs.bitcast(FP4X4),
                    lhsT_scale=lhs_scale,
                    rhs=codes[1 - op, y][:, g, :].bitcast(FP4X4),
                    rhs_scale=planes[1 - op, y][:, g, :],
                    start=(g == 0),
                    stop=(g == PASSES - 1),
                )
            made[(x, y), op, t] = acc

        def mirror(x, t):
            acc = bank()
            for n in range(TILES):
                nc.tensor.transpose(acc[:, P * n : P * (n + 1)], made[(x, x), "source", n][:, P * t : P * (t + 1)], ident[:])
            made[(x, x), "mirror", t] = acc

        def a_scaled_copy(t):
            tile = work.tile([P, BLK], F32, name="source", bufs=TILES)
            nc.scalar.activation(out=tile[:], in_=made[(A, A), PT, t][:], func=COPY, scale=v_tile[:, t : t + 1])
            made[(A, A), "source", t] = tile

        def copy_in_word_order(x, y, t):
            name, bufs = ("a_factor", TILES) if y == x else ("factor", 3)
            tile = work.tile([P, BLK], F32, name=name, bufs=bufs)
            nc.scalar.copy(out=in_word_order(tile[:]), in_=to_word_order(made[(x, y), PT, t][:]))
            made[(x, y), "factor", t] = tile

        def rows_tile(pair, t):
            made[pair, "rows", t] = work.tile([P, BLK], BF16, name="rows", bufs=2 * TILES)
            return made[pair, "rows", t]

        def a_rows(t):
            nc.vector.tensor_tensor(
                out=in_word_order(rows_tile((A, A), t)[:]),
                in0=to_word_order(made[(A, A), "mirror", t][:]),
                in1=in_word_order(made[(A, A), "factor", t][:]),
                op=MULT,
            )

        def copy_in_slot_order(x, t):
            tile = work.tile([P, BLK], F32, name="source", bufs=TILES)
            nc.scalar.copy(
                out=tile[:].rearrange("q (t p) -> q t p", t=TILES),
                in_=made[(x, x), PT, t][:].rearrange("q (p t) -> q t p", t=TILES),
            )
            made[(x, x), "source", t] = tile

        def slots_tile(pair):
            if (pair, "slots") not in made:
                made[pair, "slots"] = work.tile([P, TILES, BLK], BF16, name="slots", bufs=3)
            return made[pair, "slots"]

        def self_slot(x, t):
            nc.vector.scalar_tensor_tensor(
                out=slots_tile((x, x))[:, t, :],
                in0=made[(x, x), "mirror", t][:],
                scalar=v_slot[:, x - 1, t : t + 1],
                in1=made[(x, x), "source", t][:],
                op0=MULT,
                op1=MULT,
            )

        def bond(x, y, t):
            tile = work.tile([P, BLK], F32, name="bond", bufs=TILES)
            nc.vector.tensor_tensor(
                out=in_word_order(tile[:]),
                in0=to_word_order(made[(x, y), OV, t][:]),
                in1=in_word_order(made[(x, y), "factor", t][:]),
                op=MULT,
            )
            made[(x, y), "bond", t] = tile

        def pair_rows(x, y, t):
            nc.vector.tensor_tensor(out=rows_tile((x, y), t)[:], in0=made[(x, y), "bond", t][:], in1=v_row[y][:], op=MULT)

        def pair_slot(x, y, t):
            order = "p u e" if y == A else "u e p"
            nc.scalar.activation(
                out=slots_tile((x, y))[:, t, :].rearrange("q (%s) -> q %s" % (order, order), u=2, e=2),
                in_=made[(x, y), "bond", t][:].rearrange("q (u p e) -> q %s" % order, u=2, e=2),
                func=COPY,
                scale=v_slot[:, x - 1, t : t + 1],
            )

        def turn(pair, half):
            acc = bank()
            for n in range(2):
                words = made[pair, "rows", 2 * half + n][:].bitcast(F32)
                for u in range(2):
                    nc.tensor.transpose(acc[:, P * (2 * n + u) : P * (2 * n + u + 1)], words[:, P * u : P * (u + 1)], ident[:])
            made[pair, "turned", half] = acc

        def packed(pair, kind):
            if (pair, kind) not in made:
                made[pair, kind] = work.tile([P, TILES * BLK], BF16, name=kind, bufs=3, align_bytes=64)
            return made[pair, kind]

        def pack_turned(pair, half):
            nc.scalar.copy(
                out=packed(pair, "from_rows")[:, 2 * BLK * half : 2 * BLK * (half + 1)].bitcast(F32).rearrange("q (n r u) -> q n r u", n=2, u=2),
                in_=made[pair, "turned", half][:].rearrange("q (n u r) -> q n r u", n=2, u=2),
            )

        def pack_slots(pair, n, copy):
            copy(
                out=packed(pair, "from_slots")[:, BLK * n : BLK * (n + 1)].rearrange("q (c i t) -> q c t i", i=4, t=TILES),
                in_=made[pair, "slots"][:, :, P * n : P * (n + 1)].rearrange("q t (c i) -> q c t i", i=4),
            )

        def quantize(pair, kind, first=0, tiles=TILES):
            x, y = pair
            key = (y, x) if kind == "from_rows" else (x, y)
            cols = slice(P * first, P * (first + tiles))
            nc.vector.quantize_mx(
                out=d_codes[key][:, cols].bitcast(FP8X4),
                scales=d_planes[key][:, cols],
                in_=made[pair, kind][:, BLK * first : BLK * (first + tiles)],
            )

        def out_matmul(blk, t, first=0, width=R):
            acc = bank()[:][:, :width]
            cols = slice(first, first + width)
            for g in range(PASSES):
                nc.tensor.matmul_mx(
                    out=acc,
                    lhsT=d_codes[g, blk][:, P * t : P * (t + 1)].bitcast(FP8X4),
                    lhsT_scale=d_planes[g, blk][:, P * t : P * (t + 1)],
                    rhs=w_codes[:, g, :].bitcast(FP8X4)[:, cols],
                    rhs_scale=w_plane[:, g, cols],
                    start=(g == 0),
                    stop=(g == PASSES - 1),
                )
            made["out", blk, t, first] = acc

        def out_store(blk, t, first=0, width=R):
            cols = slice(first, first + width)
            res = work.tile([P, width], F32, name="res", bufs=8)
            nc.vector.tensor_tensor(out=res[:], in0=made["out", blk, t, first], in1=b_row[:, cols], op=ADD)
            rows = out[BLK * blk : BLK * (blk + 1), cols]
            dst = rows[P * t : P * (t + 1), :] if blk == A else rows.rearrange("(p t) r -> t p r", t=TILES)[t]
            nc.sync.dma_start(out=dst, in_=res[:])

        def pair_step(x, y, t):
            product(PT, x, y, t)
            product(OV, x, y, t)
            copy_in_word_order(x, y, t)
            if t > 0:
                pair_slot(x, y, t - 1)

        on_scalar, on_vector = nc.scalar.copy, nc.vector.tensor_copy


        aa, ba, bb, bc, cc, ca = (A, A), (B, A), (B, B), (B, C), (C, C), (C, A)
        for t in range(TILES):
            product(PT, A, A, t)
            a_scaled_copy(t)
            if t == 0:
                copy_in_word_order(A, A, t)
        gather_codes(PT, B, 0)
        gather_codes(OV, B, 0)
        gather_scales(PT, B, 0)
        gather_codes(PT, B, 2)
        gather_scales(OV, B, 0)
        gather_codes(OV, B, 2)
        gather_scales(PT, B, 2)
        gather_scales(OV, B, 2)

        product(PT, B, A, 0)
        for t in range(1, TILES):
            copy_in_word_order(A, A, t)
        nc.scalar.activation(out=v_slot[:], in_=v_slot16[:], func=COPY)
        copy_in_word_order(B, A, 0)
        spread = bank()
        for t in range(TILES):
            nc.tensor.transpose(spread[:, P * t : P * (t + 1)], v_tile[:, t : t + 1].to_broadcast([P, P]), ident[:])
        v_row[A] = keep.tile([P, BLK], F32, name="v_row_a")
        nc.scalar.copy(out=in_word_order(v_row[A][:]), in_=to_word_order(spread[:]))
        for t in range(TILES):
            mirror(A, t)
        a_rows(0)
        product(OV, B, A, 0)
        a_rows(1)
        bond(B, A, 0)
        pair_step(B, A, 1)
        a_rows(2)
        a_rows(3)
        bond(B, A, 1)
        pair_rows(B, A, 0)
        pair_step(B, A, 2)
        pair_rows(B, A, 1)
        turn(aa, 0)
        turn(aa, 1)
        bond(B, A, 2)
        pack_turned(aa, 0)
        pack_turned(aa, 1)
        gather_next_of_c()
        pair_step(B, A, 3)
        v_row[C] = keep.tile([P, BLK], F32, name="v_row_c")
        nc.scalar.copy(out=in_word_order(v_row[C][:]), in_=to_word_order(v_c16[:]))
        pair_rows(B, A, 2)
        quantize(aa, "from_rows")
        gather_next_of_c()
        bond(B, A, 3)

        def self_step(x, t):
            product(PT, x, x, t)
            copy_in_slot_order(x, t)

        def first_steps(x, y, last, own, early_pack):
            pair_step(x, y, 0)
            pack_slots(last, 0, early_pack)
            pack_slots(last, 1, early_pack)
            gather_next_of_c()
            turn(last, 0)
            turn(last, 1)
            for t in range(TILES):
                mirror(own, t)
            pack_turned(last, 0)
            pack_turned(last, 1)
            bond(x, y, 0)
            self_slot(own, 0)
            self_slot(own, 1)
            pair_step(x, y, 1)
            pack_slots(last, 2, on_scalar)
            self_slot(own, 2)
            self_slot(own, 3)
            bond(x, y, 1)
            quantize(last, "from_rows")
            pair_rows(x, y, 0)
            pack_slots(last, 3, on_scalar)
            pair_step(x, y, 2)
            pack_slots((own, own), 0, on_scalar)
            pair_rows(x, y, 1)
            bond(x, y, 2)
            quantize(last, "from_slots")

        for t in range(TILES):
            self_step(B, t)
            if t == 0:
                pair_slot(B, A, 3)
            gather_next_of_c()
            if t == 0:
                pair_rows(B, A, 3)

        first_steps(B, C, ba, B, on_scalar)
        pack_slots(bb, 1, on_scalar)
        pair_step(B, C, 3)
        pair_rows(B, C, 2)
        bond(B, C, 3)

        self_step(C, 0)
        pair_slot(B, C, 3)
        gather_next_of_c()
        pair_rows(B, C, 3)
        self_step(C, 1)
        pack_slots(bb, 2, on_vector)
        pack_slots(bb, 3, on_vector)
        quantize(bb, "from_slots")
        self_step(C, 2)
        self_step(C, 3)

        first_steps(C, A, bc, C, on_vector)
        out_matmul(B, 0)
        out_store(B, 0)
        pack_slots(cc, 1, on_scalar)
        out_matmul(B, 1)
        turn(ca, 0)
        pack_turned(ca, 0)
        out_store(B, 1)
        pair_step(C, A, 3)
        pair_rows(C, A, 2)
        quantize(cc, "from_slots", 0, 2)
        quantize(ca, "from_rows", 0, 2)
        bond(C, A, 3)

        pair_slot(C, A, 3)
        out_matmul(B, 2)
        pair_rows(C, A, 3)
        out_matmul(B, 3)
        pack_slots(ca, 0, on_scalar)
        pack_slots(ca, 1, on_vector)
        out_store(B, 2)
        out_matmul(C, 0)
        turn(ca, 1)
        pack_slots(ca, 2, on_scalar)
        quantize(ca, "from_slots", 0, 2)
        out_store(B, 3)
        out_matmul(C, 1)
        pack_slots(ca, 3, on_scalar)
        pack_turned(ca, 1)
        pack_slots(cc, 2, on_scalar)
        pack_slots(cc, 3, on_scalar)
        out_store(C, 0)
        out_matmul(A, 0)
        quantize(ca, "from_slots", 2, 2)
        out_store(C, 1)
        out_matmul(A, 1)
        quantize(ca, "from_rows", 2, 2)
        out_store(A, 0)
        quantize(cc, "from_slots", 2, 2)
        rest = [(A, 1), (A, 2), (A, 3), (C, 2), (C, 3, 0, R // 2), (C, 3, R // 2, R // 2)]
        for n in range(1, len(rest)):
            out_matmul(*rest[n])
            out_store(*rest[n - 1])
        out_store(*rest[-1])
